import numpy as np
import ml_dtypes


def mxq(x, axis, fmt="e4m3"):
    dtype, down = {"e4m3": (ml_dtypes.float8_e4m3fn, 7), "e5m2": (ml_dtypes.float8_e5m2, 14)}[fmt]
    v = np.moveaxis(np.asarray(x, np.float32).astype(ml_dtypes.bfloat16).astype(np.float64), axis, -1)
    blocks = v.reshape(v.shape[:-1] + (-1, 32))
    amax = np.abs(blocks).max(-1, keepdims=True)
    byte = np.maximum(np.where(amax > 0, np.frexp(amax)[1] - 1 + 127, 0) - down, 1)
    scale = np.exp2(byte - 127.0)
    codes = (blocks / scale).astype(np.float32).astype(dtype).astype(np.float64)
    return np.moveaxis((codes * scale).reshape(v.shape), -1, axis)


WIDE = False


def mx_kscale(k):
    if not WIDE:
        return np.ones(k)
    levels = np.array([10, -10, 5, -5, 0])
    if k % 512:
        return np.exp2(np.random.permutation(np.resize(levels, k // 32))).repeat(32)
    a = np.empty((k // 512, 16))
    for p in range(k // 512):
        a[p, :8] = np.random.permutation(np.resize(levels, 8))
        for g in range(8):
            far = levels[np.abs(levels - a[p, g]) >= 10]
            a[p, g + 8] = far[np.random.randint(len(far))]
    return np.exp2(a.ravel()).repeat(32)


def f64(x):
    return np.asarray(x).astype(np.float64)


def striped(idx):
    return np.tile(np.asarray(idx).reshape(-1, 16).T, (8, 1)).astype(np.uint16)


def unstriped(offs):
    return offs[:16].T.reshape(-1).astype(np.int64)


B, N, T, D, DV, NQ = 4, 256, 2048, 512, 0, 128
PAGE = 32
SEG = 32


def setup_inputs():
    n = np.random.standard_normal
    pages = np.random.permutation(T // PAGE)[:B * N // PAGE]
    idx = (pages[:, None] * PAGE + np.arange(PAGE)[None, :]).reshape(-1)
    s = mx_kscale(D)[:, None]
    r = np.random.uniform(0.5, 2.0, T)
    return {
        "qT": (n((B, D, NQ)) * s * (1.00 / np.sqrt(D))).astype(np.float32),
        "kT": (n((D, T)) / s / r).astype(np.float32),
        "ts": np.tile(r, (128, 1)).astype(np.float32),
        "kb": np.tile(n(T), (128, 1)).astype(np.float32),
        "offs": striped(idx),
    }


def reference(qT, kT, ts, kb, offs):
    idx = unstriped(offs)
    pick = lambda x: x[:, idx].reshape(x.shape[0], B, N).transpose(1, 0, 2)
    a = mxq(f64(qT), 1, "e4m3").transpose(0, 2, 1) @ mxq(pick(f64(kT)), 1, "e4m3")
    a = a * pick(f64(ts))[:, :1, :]
    a = a + pick(f64(kb))[:, :1, :]
    return a.reshape(B, NQ, N // SEG, SEG).max(-1)

@@ -1,0 +1,139 @@
+from contextlib import ExitStack
+
+import concourse.mybir as mybir
+from concourse.masks import make_identity
+
+F32 = mybir.dt.float32
+BF16 = mybir.dt.bfloat16
+U32 = mybir.dt.uint32
+U16 = mybir.dt.uint16
+U8 = mybir.dt.uint8
+FP8X4 = mybir.dt.float8_e4m3fn_x4
+COPY = mybir.ActivationFunctionType.Copy
+IDENT = mybir.ActivationFunctionType.Identity
+MAX = mybir.AluOpType.max
+X = mybir.AxisListType.X
+
+B, N, T, D, NQ = 4, 256, 2048, 512, 128
+P = 128
+FLOPS = 2 * B * NQ * N * D
+HALVES = N // P
+
+
+def tile_attend_maxsim_tskb_kernel(tc, qT, kT, ts, kb, offs, out):
+    nc = tc.nc
+    with ExitStack() as ctx:
+        held = ctx.enter_context(tc.tile_pool(name="held", bufs=1))
+        psum_mm = ctx.enter_context(tc.psum_pool(name="psum_mm", bufs=4))
+        psum_t = ctx.enter_context(tc.psum_pool(name="psum_t", bufs=2))
+        psum_c = ctx.enter_context(tc.psum_pool(name="psum_c", bufs=2))
+        work = ctx.enter_context(tc.tile_pool(name="work", bufs=4))
+
+        offsets = held.tile([P, B * N // 16], U16, name="offsets")
+        nc.sync.dma_start(offsets[:], offs)
+
+        ts_win = held.tile([P, T], F32, name="ts_win")
+        kb_win = held.tile([P, T], F32, name="kb_win")
+        nc.vector.memset(ts_win[:], 0.0)
+        nc.gpsimd.memset(kb_win[:], 0.0)
+
+        k_rows = kT.rearrange("(p t) w -> p t w", t=4)
+        planes = []
+        for t in range(4):
+            plane = held.tile([P, T], F32, name="plane%d" % t)
+            nc.sync.dma_start(plane[:], k_rows[:, t, :])
+            if t == 0:
+                nc.sync.dma_start(ts_win[0:1, :], ts[0:1, :])
+                nc.sync.dma_start(kb_win[0:1, :], kb[0:1, :])
+            planes.append(plane)
+
+        q_raws = []
+        for h in range(2):
+            q_raw = held.tile([P, 2, 4 * NQ], F32, name="q_raw%d" % h)
+            nc.sync.dma_start(q_raw[:], qT[2 * h : 2 * h + 2].rearrange("b (p t) q -> p b (t q)", t=4))
+            q_raws.append(q_raw)
+
+        ident = held.tile([P, P], F32, name="ident")
+        make_identity(nc, ident[:])
+
+        warm = held.tile([P, 8], F32, name="warm")
+        nc.vector.memset(warm[:], 0.0)
+        warm2 = held.tile([P, 8], F32, name="warm2")
+        nc.scalar.activation(warm2[:], warm[:], IDENT)
+
+        cols = []
+        for name, win in (("ts", ts_win), ("kb", kb_win)):
+            picked = held.tile([P, B * N], F32, name=name + "_picked")
+            nc.vector.tensor_copy(picked[:], win[:].indirect(offsets[:]))
+            col = held.tile([P, 8], F32, name=name + "_col")
+            for half in range(2):
+                bank = psum_c.tile([P, 4, P], F32, name="bank_c")
+                for j in range(4):
+                    k = 4 * half + j
+                    nc.tensor.transpose(bank[:, j, :], picked[:, k * P : (k + 1) * P], ident[:])
+                nc.scalar.copy(col[:, 4 * half : 4 * half + 4], bank[:, :, 0])
+            cols.append(col)
+        ts_col, kb_col = cols
+
+        raw = held.tile([P, 4, B * N], F32, name="raw")
+        grouped = [held.tile([P, N, 4], BF16, name="grouped%d" % b, align_bytes=64) for b in range(B)]
+        for t in range(3):
+            nc.vector.tensor_copy(raw[:, t, :], planes[t][:].indirect(offsets[:]))
+        for b in range(B):
+            nc.scalar.activation(grouped[b][:, :, 0:2], raw[:, 0:2, b * N : (b + 1) * N].rearrange("p t n -> p n t"), COPY)
+        for b in range(B):
+            nc.vector.tensor_copy(
+                raw[:, 3, b * N : (b + 1) * N],
+                planes[3][:].indirect(offsets[:, b * (N // 16) : (b + 1) * (N // 16)]),
+            )
+        k_codes, k_scales = [], []
+        q_codes, q_scales = [], []
+        for b in range(B):
+            src = raw[:, 2:4, b * N : (b + 1) * N].rearrange("p t n -> p n t")
+            if b % 2 == 0:
+                nc.scalar.activation(grouped[b][:, :, 2:4], src, COPY)
+            else:
+                nc.vector.tensor_copy(grouped[b][:, :, 2:4], src)
+            if b % 2 == 0:
+                h = b // 2
+                q_grouped = held.tile([P, 2, NQ, 4], BF16, name="q_grouped%d" % h, align_bytes=64)
+                nc.scalar.activation(
+                    q_grouped[:], q_raws[h][:].rearrange("p b (t q) -> p b q t", t=4), COPY
+                )
+                qc = held.tile([P, 2 * NQ], U32, name="q_codes%d" % h, align_bytes=64)
+                qs = held.tile([P, 2 * NQ], U8, name="q_scales%d" % h, align_bytes=64)
+                nc.vector.quantize_mx(
+                    out=qc[:].bitcast(FP8X4), scales=qs[:], in_=q_grouped[:].rearrange("p b q t -> p (b q t)")
+                )
+                q_codes.append(qc)
+                q_scales.append(qs)
+            kc = held.tile([P, N], U32, name="k_codes%d" % b, align_bytes=64)
+            ks = held.tile([P, N], U8, name="k_scales%d" % b, align_bytes=64)
+            nc.vector.quantize_mx(
+                out=kc[:].bitcast(FP8X4), scales=ks[:], in_=grouped[b][:].rearrange("p n t -> p (n t)")
+            )
+            k_codes.append(kc)
+            k_scales.append(ks)
+
+        for b in range(B):
+            turned = psum_t.tile([P, N], F32, name="turned")
+            q_cols = slice((b % 2) * NQ, (b % 2 + 1) * NQ)
+            for half in range(HALVES):
+                acc = psum_mm.tile([P, NQ], F32, name="acc")
+                s_cols = slice(half * P, (half + 1) * P)
+                nc.tensor.matmul_mx(
+                    out=acc[:],
+                    lhsT=k_codes[b][:, s_cols].bitcast(FP8X4),
+                    lhsT_scale=k_scales[b][:, s_cols],
+                    rhs=q_codes[b // 2][:, q_cols].bitcast(FP8X4),
+                    rhs_scale=q_scales[b // 2][:, q_cols],
+                    start=True,
+                    stop=True,
+                )
+                k = HALVES * b + half
+                scored = work.tile([P, NQ], F32, name="scored")
+                nc.scalar.activation(scored[:], acc[:], IDENT, bias=kb_col[:, k : k + 1], scale=ts_col[:, k : k + 1])
+                nc.tensor.transpose(turned[:, s_cols], scored[:], ident[:])
+            best = work.tile([P, N // 32], F32, name="best")
+            nc.vector.tensor_reduce(out=best[:], in_=turned[:].rearrange("p (j s) -> p j s", s=32), axis=X, op=MAX)
+            nc.sync.dma_start(out[b], best[:])

@@ -18,33 +18,32 @@ B, N, T, D, NQ = 4, 256, 2048, 512, 128
 P = 128
 FLOPS = 2 * B * NQ * N * D
 HALVES = N // P
+LIST_COLS = N // 16
+TS_ROW, KB_ROW = 0, 64
+PLACED_ON_SCALAR = 3
 
 
 def tile_attend_maxsim_tskb_kernel(tc, qT, kT, ts, kb, offs, out):
     nc = tc.nc
     with ExitStack() as ctx:
         held = ctx.enter_context(tc.tile_pool(name="held", bufs=1))
-        psum_mm = ctx.enter_context(tc.psum_pool(name="psum_mm", bufs=4))
-        psum_t = ctx.enter_context(tc.psum_pool(name="psum_t", bufs=2))
+        shared = ctx.enter_context(tc.tile_pool(name="shared", bufs=1))
+        psum_mm = ctx.enter_context(tc.psum_pool(name="psum_mm", bufs=3))
+        psum_t = ctx.enter_context(tc.psum_pool(name="psum_t", bufs=3))
         psum_c = ctx.enter_context(tc.psum_pool(name="psum_c", bufs=2))
-        work = ctx.enter_context(tc.tile_pool(name="work", bufs=4))
+        work = ctx.enter_context(tc.tile_pool(name="work", bufs=8))
 
-        offsets = held.tile([P, B * N // 16], U16, name="offsets")
+        offsets = held.tile([P, B * LIST_COLS], U16, name="offsets")
         nc.sync.dma_start(offsets[:], offs)
 
-        ts_win = held.tile([P, T], F32, name="ts_win")
-        kb_win = held.tile([P, T], F32, name="kb_win")
-        nc.vector.memset(ts_win[:], 0.0)
-        nc.gpsimd.memset(kb_win[:], 0.0)
+        def listed(b):
+            return offsets[:, b * LIST_COLS : (b + 1) * LIST_COLS]
 
         k_rows = kT.rearrange("(p t) w -> p t w", t=4)
         planes = []
         for t in range(4):
-            plane = held.tile([P, T], F32, name="plane%d" % t)
+            plane = held.tile([P, T], F32, name="plane%d" % t, tag="plane%d" % t)
             nc.sync.dma_start(plane[:], k_rows[:, t, :])
-            if t == 0:
-                nc.sync.dma_start(ts_win[0:1, :], ts[0:1, :])
-                nc.sync.dma_start(kb_win[0:1, :], kb[0:1, :])
             planes.append(plane)
 
         q_raws = []
@@ -53,76 +52,88 @@ def tile_attend_maxsim_tskb_kernel(tc, qT, kT, ts, kb, offs, out):
             nc.sync.dma_start(q_raw[:], qT[2 * h : 2 * h + 2].rearrange("b (p t) q -> p b (t q)", t=4))
             q_raws.append(q_raw)
 
+        ts_win = shared.tile([P, T], F32, name="ts_win", offset=0)
+        kb_win = held.tile([P, T], F32, name="kb_win")
+        nc.vector.memset(ts_win[:], 0.0)
+        nc.vector.memset(kb_win[:], 0.0)
+        nc.scalar.dma_start(ts_win[TS_ROW : TS_ROW + 1, :], ts[0:1, :])
+        nc.scalar.dma_start(kb_win[KB_ROW : KB_ROW + 1, :], kb[0:1, :])
+
         ident = held.tile([P, P], F32, name="ident")
         make_identity(nc, ident[:])
 
-        warm = held.tile([P, 8], F32, name="warm")
-        nc.vector.memset(warm[:], 0.0)
-        warm2 = held.tile([P, 8], F32, name="warm2")
-        nc.scalar.activation(warm2[:], warm[:], IDENT)
-
-        cols = []
-        for name, win in (("ts", ts_win), ("kb", kb_win)):
-            picked = held.tile([P, B * N], F32, name=name + "_picked")
-            nc.vector.tensor_copy(picked[:], win[:].indirect(offsets[:]))
+        def to_columns(name, picked, row):
             col = held.tile([P, 8], F32, name=name + "_col")
             for half in range(2):
                 bank = psum_c.tile([P, 4, P], F32, name="bank_c")
                 for j in range(4):
                     k = 4 * half + j
                     nc.tensor.transpose(bank[:, j, :], picked[:, k * P : (k + 1) * P], ident[:])
-                nc.scalar.copy(col[:, 4 * half : 4 * half + 4], bank[:, :, 0])
-            cols.append(col)
-        ts_col, kb_col = cols
+                nc.scalar.copy(col[:, 4 * half : 4 * half + 4], bank[:, :, row])
+            return col
 
-        raw = held.tile([P, 4, B * N], F32, name="raw")
+        ts_picked = held.tile([P, B * N], F32, name="ts_picked")
+        nc.vector.tensor_copy(ts_picked[:], ts_win[:].indirect(offsets[:]))
+        ts_col = to_columns("ts", ts_picked, TS_ROW)
+
         grouped = [held.tile([P, N, 4], BF16, name="grouped%d" % b, align_bytes=64) for b in range(B)]
-        for t in range(3):
-            nc.vector.tensor_copy(raw[:, t, :], planes[t][:].indirect(offsets[:]))
+        low = [shared.tile([P, 2, N], F32, name="low%d" % b, offset=b * 2 * N * 4) for b in range(B)]
+        high = [held.tile([P, 2, N], F32, name="high%d" % b) for b in range(B)]
         for b in range(B):
-            nc.scalar.activation(grouped[b][:, :, 0:2], raw[:, 0:2, b * N : (b + 1) * N].rearrange("p t n -> p n t"), COPY)
+            nc.vector.tensor_copy(low[b][:, 0, :], planes[0][:].indirect(listed(b)))
         for b in range(B):
-            nc.vector.tensor_copy(
-                raw[:, 3, b * N : (b + 1) * N],
-                planes[3][:].indirect(offsets[:, b * (N // 16) : (b + 1) * (N // 16)]),
-            )
-        k_codes, k_scales = [], []
-        q_codes, q_scales = [], []
+            nc.vector.tensor_copy(low[b][:, 1, :], planes[1][:].indirect(listed(b)))
+            nc.scalar.activation(grouped[b][:, :, 0:2], low[b][:].rearrange("p t n -> p n t"), COPY)
+
+        kb_picked = held.tile([P, B * N], F32, name="kb_picked", tag="plane1")
+        nc.vector.tensor_copy(kb_picked[:], kb_win[:].indirect(offsets[:]))
+        kb_col = to_columns("kb", kb_picked, KB_ROW)
+
+        for t in (2, 3):
+            for b in range(B):
+                nc.vector.tensor_copy(high[b][:, t - 2, :], planes[t][:].indirect(listed(b)))
         for b in range(B):
-            src = raw[:, 2:4, b * N : (b + 1) * N].rearrange("p t n -> p n t")
-            if b % 2 == 0:
+            src = high[b][:].rearrange("p t n -> p n t")
+            if b < PLACED_ON_SCALAR:
                 nc.scalar.activation(grouped[b][:, :, 2:4], src, COPY)
             else:
                 nc.vector.tensor_copy(grouped[b][:, :, 2:4], src)
-            if b % 2 == 0:
-                h = b // 2
-                q_grouped = held.tile([P, 2, NQ, 4], BF16, name="q_grouped%d" % h, align_bytes=64)
-                nc.scalar.activation(
-                    q_grouped[:], q_raws[h][:].rearrange("p b (t q) -> p b q t", t=4), COPY
-                )
-                qc = held.tile([P, 2 * NQ], U32, name="q_codes%d" % h, align_bytes=64)
-                qs = held.tile([P, 2 * NQ], U8, name="q_scales%d" % h, align_bytes=64)
-                nc.vector.quantize_mx(
-                    out=qc[:].bitcast(FP8X4), scales=qs[:], in_=q_grouped[:].rearrange("p b q t -> p (b q t)")
-                )
-                q_codes.append(qc)
-                q_scales.append(qs)
-            kc = held.tile([P, N], U32, name="k_codes%d" % b, align_bytes=64)
-            ks = held.tile([P, N], U8, name="k_scales%d" % b, align_bytes=64)
+
+        q_codes, q_scales = [], []
+        k_codes, k_scales = [], []
+        for h in range(2):
+            q_grouped = held.tile([P, 2, NQ, 4], BF16, name="q_grouped%d" % h, align_bytes=64)
+            for j in range(2):
+                dst = q_grouped[:, j, :, :].rearrange("p (c i) t -> p c t i", i=4)
+                src = q_raws[h][:, j, :].rearrange("p (t c i) -> p c t i", t=4, i=4)
+                if h == 0:
+                    nc.vector.tensor_copy(dst, src)
+                else:
+                    nc.scalar.activation(dst, src, COPY)
+            qc = held.tile([P, 2 * NQ], U32, name="q_codes%d" % h, align_bytes=64)
+            qs = held.tile([P, 2 * NQ], U8, name="q_scales%d" % h, align_bytes=64)
             nc.vector.quantize_mx(
-                out=kc[:].bitcast(FP8X4), scales=ks[:], in_=grouped[b][:].rearrange("p n t -> p (n t)")
+                out=qc[:].bitcast(FP8X4), scales=qs[:], in_=q_grouped[:].rearrange("p b q t -> p (b q t)")
             )
-            k_codes.append(kc)
-            k_scales.append(ks)
+            q_codes.append(qc)
+            q_scales.append(qs)
+            for b in (2 * h, 2 * h + 1):
+                kc = held.tile([P, N], U32, name="k_codes%d" % b, align_bytes=64)
+                ks = held.tile([P, N], U8, name="k_scales%d" % b, align_bytes=64)
+                nc.vector.quantize_mx(
+                    out=kc[:].bitcast(FP8X4), scales=ks[:], in_=grouped[b][:].rearrange("p n t -> p (n t)")
+                )
+                k_codes.append(kc)
+                k_scales.append(ks)
 
         for b in range(B):
+            acc = psum_mm.tile([P, HALVES, NQ], F32, name="acc")
             turned = psum_t.tile([P, N], F32, name="turned")
             q_cols = slice((b % 2) * NQ, (b % 2 + 1) * NQ)
             for half in range(HALVES):
-                acc = psum_mm.tile([P, NQ], F32, name="acc")
                 s_cols = slice(half * P, (half + 1) * P)
                 nc.tensor.matmul_mx(
-                    out=acc[:],
+                    out=acc[:, half, :],
                     lhsT=k_codes[b][:, s_cols].bitcast(FP8X4),
                     lhsT_scale=k_scales[b][:, s_cols],
                     rhs=q_codes[b // 2][:, q_cols].bitcast(FP8X4),
@@ -130,10 +141,13 @@ def tile_attend_maxsim_tskb_kernel(tc, qT, kT, ts, kb, offs, out):
                     start=True,
                     stop=True,
                 )
+            for half in range(HALVES):
                 k = HALVES * b + half
                 scored = work.tile([P, NQ], F32, name="scored")
-                nc.scalar.activation(scored[:], acc[:], IDENT, bias=kb_col[:, k : k + 1], scale=ts_col[:, k : k + 1])
-                nc.tensor.transpose(turned[:, s_cols], scored[:], ident[:])
+                nc.scalar.activation(
+                    scored[:], acc[:, half, :], IDENT, bias=kb_col[:, k : k + 1], scale=ts_col[:, k : k + 1]
+                )
+                nc.tensor.transpose(turned[:, half * P : (half + 1) * P], scored[:], ident[:])
             best = work.tile([P, N // 32], F32, name="best")
             nc.vector.tensor_reduce(out=best[:], in_=turned[:].rearrange("p (j s) -> p j s", s=32), axis=X, op=MAX)
             nc.sync.dma_start(out[b], best[:])

@@ -20,14 +20,15 @@ FLOPS = 2 * B * NQ * N * D
 HALVES = N // P
 LIST_COLS = N // 16
 TS_ROW, KB_ROW = 0, 64
-PLACED_ON_SCALAR = 3
+CHUNKS = (((512, 0), (512, 0), (1024, 0)), ((1024, 0), (512, 512), (512, 384)))
+WOVEN_ON_SCALAR = 4
+I32 = mybir.dt.int32
 
 
 def tile_attend_maxsim_tskb_kernel(tc, qT, kT, ts, kb, offs, out):
     nc = tc.nc
     with ExitStack() as ctx:
         held = ctx.enter_context(tc.tile_pool(name="held", bufs=1))
-        shared = ctx.enter_context(tc.tile_pool(name="shared", bufs=1))
         psum_mm = ctx.enter_context(tc.psum_pool(name="psum_mm", bufs=3))
         psum_t = ctx.enter_context(tc.psum_pool(name="psum_t", bufs=3))
         psum_c = ctx.enter_context(tc.psum_pool(name="psum_c", bufs=2))
@@ -39,12 +40,24 @@ def tile_attend_maxsim_tskb_kernel(tc, qT, kT, ts, kb, offs, out):
         def listed(b):
             return offsets[:, b * LIST_COLS : (b + 1) * LIST_COLS]
 
-        k_rows = kT.rearrange("(p t) w -> p t w", t=4)
-        planes = []
-        for t in range(4):
-            plane = held.tile([P, T], F32, name="plane%d" % t, tag="plane%d" % t)
-            nc.sync.dma_start(plane[:], k_rows[:, t, :])
-            planes.append(plane)
+        ts_win = held.tile([P, T], F32, name="ts_win")
+        kb_win = held.tile([P, T], F32, name="kb_win")
+        nc.vector.memset(ts_win[:], 0.0)
+        nc.vector.memset(kb_win[:], 0.0)
+
+        k_rows = kT.rearrange("(p u e) w -> p u e w", u=2, e=2)
+        chunks = []
+        for u in range(2):
+            first = 0
+            for c, (width, on_vector) in enumerate(CHUNKS[u]):
+                raw = held.tile([P, 2, width], F32, name="raw%d_%d" % (u, c))
+                nc.sync.dma_start(raw[:], k_rows[:, u, :, first : first + width])
+                if (u, c) == (0, 0):
+                    nc.sync.dma_start(ts_win[TS_ROW : TS_ROW + 1, :], ts[0:1, :])
+                if (u, c) == (0, 1):
+                    nc.sync.dma_start(kb_win[KB_ROW : KB_ROW + 1, :], kb[0:1, :])
+                chunks.append((u, raw, first, width, on_vector))
+                first = first + width
 
         q_raws = []
         for h in range(2):
@@ -52,12 +65,6 @@ def tile_attend_maxsim_tskb_kernel(tc, qT, kT, ts, kb, offs, out):
             nc.sync.dma_start(q_raw[:], qT[2 * h : 2 * h + 2].rearrange("b (p t) q -> p b (t q)", t=4))
             q_raws.append(q_raw)
 
-        ts_win = shared.tile([P, T], F32, name="ts_win", offset=0)
-        kb_win = held.tile([P, T], F32, name="kb_win")
-        nc.vector.memset(ts_win[:], 0.0)
-        nc.vector.memset(kb_win[:], 0.0)
-        nc.scalar.dma_start(ts_win[TS_ROW : TS_ROW + 1, :], ts[0:1, :])
-        nc.scalar.dma_start(kb_win[KB_ROW : KB_ROW + 1, :], kb[0:1, :])
 
         ident = held.tile([P, P], F32, name="ident")
         make_identity(nc, ident[:])
@@ -76,28 +83,38 @@ def tile_attend_maxsim_tskb_kernel(tc, qT, kT, ts, kb, offs, out):
         nc.vector.tensor_copy(ts_picked[:], ts_win[:].indirect(offsets[:]))
         ts_col = to_columns("ts", ts_picked, TS_ROW)
 
-        grouped = [held.tile([P, N, 4], BF16, name="grouped%d" % b, align_bytes=64) for b in range(B)]
-        low = [shared.tile([P, 2, N], F32, name="low%d" % b, offset=b * 2 * N * 4) for b in range(B)]
-        high = [held.tile([P, 2, N], F32, name="high%d" % b) for b in range(B)]
-        for b in range(B):
-            nc.vector.tensor_copy(low[b][:, 0, :], planes[0][:].indirect(listed(b)))
-        for b in range(B):
-            nc.vector.tensor_copy(low[b][:, 1, :], planes[1][:].indirect(listed(b)))
-            nc.scalar.activation(grouped[b][:, :, 0:2], low[b][:].rearrange("p t n -> p n t"), COPY)
-
-        kb_picked = held.tile([P, B * N], F32, name="kb_picked", tag="plane1")
+        kb_picked = held.tile([P, B * N], F32, name="kb_picked")
         nc.vector.tensor_copy(kb_picked[:], kb_win[:].indirect(offsets[:]))
         kb_col = to_columns("kb", kb_picked, KB_ROW)
 
-        for t in (2, 3):
+        pools = [held.tile([P, T, 2], BF16, name="pool%d" % u) for u in range(2)]
+        picked = [held.tile([P, 2, N], U32, name="picked%d" % b) for b in range(B)]
+        grouped = [held.tile([P, N, 4], BF16, name="grouped%d" % b, align_bytes=64) for b in range(B)]
+        for u in range(2):
+            for pair, raw, first, width, on_vector in chunks:
+                if pair != u:
+                    continue
+                split = width - on_vector
+                for lo, hi in ((0, split), (split, width)):
+                    if lo == hi:
+                        continue
+                    dst = pools[u][:, first + lo : first + hi, :].rearrange("p (c i) e -> p c e i", i=4)
+                    src = raw[:, :, lo:hi].rearrange("p e (c i) -> p c e i", i=4)
+                    if hi == split:
+                        nc.scalar.activation(dst, src, COPY)
+                    else:
+                        nc.vector.tensor_copy(dst, src)
+            words = pools[u][:].rearrange("p w e -> p (w e)").bitcast(U32)
             for b in range(B):
-                nc.vector.tensor_copy(high[b][:, t - 2, :], planes[t][:].indirect(listed(b)))
+                nc.vector.tensor_copy(picked[b][:, u, :], words.indirect(listed(b)))
         for b in range(B):
-            src = high[b][:].rearrange("p t n -> p n t")
-            if b < PLACED_ON_SCALAR:
-                nc.scalar.activation(grouped[b][:, :, 2:4], src, COPY)
+            flat = grouped[b][:].rearrange("p n t -> p (n t)")
+            if b < WOVEN_ON_SCALAR:
+                dst = flat.bitcast(U32).rearrange("p (c i u) -> p c u i", i=4, u=2)
+                nc.scalar.copy(dst, picked[b][:].rearrange("p u (c i) -> p c u i", i=4))
             else:
-                nc.vector.tensor_copy(grouped[b][:, :, 2:4], src)
+                dst = flat.bitcast(I32).rearrange("p (c i u) -> p c u i", i=4, u=2)
+                nc.vector.tensor_copy(dst, picked[b][:].bitcast(I32).rearrange("p u (c i) -> p c u i", i=4))
 
         q_codes, q_scales = [], []
         k_codes, k_scales = [], []

@@ -21,7 +21,9 @@ HALVES = N // P
 LIST_COLS = N // 16
 TS_ROW, KB_ROW = 0, 64
 CHUNKS = (((512, 0), (512, 0), (1024, 0)), ((1024, 0), (512, 512), (512, 384)))
-WOVEN_ON_SCALAR = 4
+WOVEN_ON_VECTOR = 2
+QUERIES_ON_VECTOR = 0
+SEARCH_BYTES = 2048
 I32 = mybir.dt.int32
 
 
@@ -29,10 +31,8 @@ def tile_attend_maxsim_tskb_kernel(tc, qT, kT, ts, kb, offs, out):
     nc = tc.nc
     with ExitStack() as ctx:
         held = ctx.enter_context(tc.tile_pool(name="held", bufs=1))
-        psum_mm = ctx.enter_context(tc.psum_pool(name="psum_mm", bufs=3))
-        psum_t = ctx.enter_context(tc.psum_pool(name="psum_t", bufs=3))
-        psum_c = ctx.enter_context(tc.psum_pool(name="psum_c", bufs=2))
-        work = ctx.enter_context(tc.tile_pool(name="work", bufs=8))
+        shared = ctx.enter_context(tc.tile_pool(name="shared", bufs=1))
+        psum = ctx.enter_context(tc.psum_pool(name="psum", bufs=8))
 
         offsets = held.tile([P, B * LIST_COLS], U16, name="offsets")
         nc.sync.dma_start(offsets[:], offs)
@@ -50,7 +50,7 @@ def tile_attend_maxsim_tskb_kernel(tc, qT, kT, ts, kb, offs, out):
         for u in range(2):
             first = 0
             for c, (width, on_vector) in enumerate(CHUNKS[u]):
-                raw = held.tile([P, 2, width], F32, name="raw%d_%d" % (u, c))
+                raw = held.tile([P, 2, width], F32, name="raw%d_%d" % (u, c), tag="raw%d_%d" % (u, c))
                 nc.sync.dma_start(raw[:], k_rows[:, u, :, first : first + width])
                 if (u, c) == (0, 0):
                     nc.sync.dma_start(ts_win[TS_ROW : TS_ROW + 1, :], ts[0:1, :])
@@ -61,35 +61,26 @@ def tile_attend_maxsim_tskb_kernel(tc, qT, kT, ts, kb, offs, out):
 
         q_raws = []
         for h in range(2):
-            q_raw = held.tile([P, 2, 4 * NQ], F32, name="q_raw%d" % h)
+            q_raw = shared.tile([P, 2, 4 * NQ], F32, name="q_raw%d" % h, offset=(2 - 2 * h) * SEARCH_BYTES)
             nc.sync.dma_start(q_raw[:], qT[2 * h : 2 * h + 2].rearrange("b (p t) q -> p b (t q)", t=4))
             q_raws.append(q_raw)
-
 
         ident = held.tile([P, P], F32, name="ident")
         make_identity(nc, ident[:])
 
-        def to_columns(name, picked, row):
-            col = held.tile([P, 8], F32, name=name + "_col")
+        turned_rows = []
+        for name, win, row in (("ts", ts_win, TS_ROW), ("kb", kb_win, KB_ROW)):
+            values = held.tile([P, B * N], F32, name=name + "_picked")
+            nc.vector.tensor_copy(values[:], win[:].indirect(offsets[:]))
             for half in range(2):
-                bank = psum_c.tile([P, 4, P], F32, name="bank_c")
+                bank = psum.tile([P, 4, P], F32, name="bank", tag="bank")
                 for j in range(4):
                     k = 4 * half + j
-                    nc.tensor.transpose(bank[:, j, :], picked[:, k * P : (k + 1) * P], ident[:])
-                nc.scalar.copy(col[:, 4 * half : 4 * half + 4], bank[:, :, row])
-            return col
-
-        ts_picked = held.tile([P, B * N], F32, name="ts_picked")
-        nc.vector.tensor_copy(ts_picked[:], ts_win[:].indirect(offsets[:]))
-        ts_col = to_columns("ts", ts_picked, TS_ROW)
-
-        kb_picked = held.tile([P, B * N], F32, name="kb_picked")
-        nc.vector.tensor_copy(kb_picked[:], kb_win[:].indirect(offsets[:]))
-        kb_col = to_columns("kb", kb_picked, KB_ROW)
+                    nc.tensor.transpose(bank[:, j, :], values[:, k * P : (k + 1) * P], ident[:])
+                turned_rows.append(bank[:, :, row])
 
         pools = [held.tile([P, T, 2], BF16, name="pool%d" % u) for u in range(2)]
-        picked = [held.tile([P, 2, N], U32, name="picked%d" % b) for b in range(B)]
-        grouped = [held.tile([P, N, 4], BF16, name="grouped%d" % b, align_bytes=64) for b in range(B)]
+        picked = [shared.tile([P, 2, N], U32, name="picked%d" % b, offset=(B + b) * SEARCH_BYTES) for b in range(B)]
         for u in range(2):
             for pair, raw, first, width, on_vector in chunks:
                 if pair != u:
@@ -107,9 +98,24 @@ def tile_attend_maxsim_tskb_kernel(tc, qT, kT, ts, kb, offs, out):
             words = pools[u][:].rearrange("p w e -> p (w e)").bitcast(U32)
             for b in range(B):
                 nc.vector.tensor_copy(picked[b][:, u, :], words.indirect(listed(b)))
+        cols = held.tile([P, 16], F32, name="cols", tag="raw1_2")
+        for i, turned_row in enumerate(turned_rows):
+            nc.scalar.copy(cols[:, 4 * i : 4 * i + 4], turned_row)
+        q_grouped = [held.tile([P, 2, NQ, 4], BF16, name="q_grouped%d" % h, align_bytes=64) for h in range(2)]
+        for b in range(B):
+            dst = q_grouped[b // 2][:, b % 2, :, :].rearrange("p (c i) t -> p c t i", i=4)
+            src = q_raws[b // 2][:, b % 2, :].rearrange("p (t c i) -> p c t i", t=4, i=4)
+            if b < QUERIES_ON_VECTOR:
+                nc.vector.tensor_copy(dst, src)
+            else:
+                nc.scalar.activation(dst, src, COPY)
+        grouped = [held.tile([P, N, 4], BF16, name="grouped%d" % b, align_bytes=64) for b in range(2)] + [
+            shared.tile([P, N, 4], BF16, name="grouped%d" % b, align_bytes=64, offset=(b - 2) * SEARCH_BYTES)
+            for b in range(2, B)
+        ]
         for b in range(B):
             flat = grouped[b][:].rearrange("p n t -> p (n t)")
-            if b < WOVEN_ON_SCALAR:
+            if b >= WOVEN_ON_VECTOR:
                 dst = flat.bitcast(U32).rearrange("p (c i u) -> p c u i", i=4, u=2)
                 nc.scalar.copy(dst, picked[b][:].rearrange("p u (c i) -> p c u i", i=4))
             else:
@@ -119,18 +125,10 @@ def tile_attend_maxsim_tskb_kernel(tc, qT, kT, ts, kb, offs, out):
         q_codes, q_scales = [], []
         k_codes, k_scales = [], []
         for h in range(2):
-            q_grouped = held.tile([P, 2, NQ, 4], BF16, name="q_grouped%d" % h, align_bytes=64)
-            for j in range(2):
-                dst = q_grouped[:, j, :, :].rearrange("p (c i) t -> p c t i", i=4)
-                src = q_raws[h][:, j, :].rearrange("p (t c i) -> p c t i", t=4, i=4)
-                if h == 0:
-                    nc.vector.tensor_copy(dst, src)
-                else:
-                    nc.scalar.activation(dst, src, COPY)
             qc = held.tile([P, 2 * NQ], U32, name="q_codes%d" % h, align_bytes=64)
             qs = held.tile([P, 2 * NQ], U8, name="q_scales%d" % h, align_bytes=64)
             nc.vector.quantize_mx(
-                out=qc[:].bitcast(FP8X4), scales=qs[:], in_=q_grouped[:].rearrange("p b q t -> p (b q t)")
+                out=qc[:].bitcast(FP8X4), scales=qs[:], in_=q_grouped[h][:].rearrange("p b q t -> p (b q t)")
             )
             q_codes.append(qc)
             q_scales.append(qs)
@@ -143,9 +141,10 @@ def tile_attend_maxsim_tskb_kernel(tc, qT, kT, ts, kb, offs, out):
                 k_codes.append(kc)
                 k_scales.append(ks)
 
+        accs = []
         for b in range(B):
-            acc = psum_mm.tile([P, HALVES, NQ], F32, name="acc")
-            turned = psum_t.tile([P, N], F32, name="turned")
+            acc = psum.tile([P, HALVES, NQ], F32, name="acc", tag="bank")
+            accs.append(acc)
             q_cols = slice((b % 2) * NQ, (b % 2 + 1) * NQ)
             for half in range(HALVES):
                 s_cols = slice(half * P, (half + 1) * P)
@@ -158,13 +157,15 @@ def tile_attend_maxsim_tskb_kernel(tc, qT, kT, ts, kb, offs, out):
                     start=True,
                     stop=True,
                 )
+        for b in range(B):
+            turned = psum.tile([P, N], F32, name="turned", tag="bank")
             for half in range(HALVES):
                 k = HALVES * b + half
-                scored = work.tile([P, NQ], F32, name="scored")
+                scored = shared.tile([P, NQ], F32, name="scored%d" % k, offset=(2 * B - 1) * SEARCH_BYTES + k * NQ * 4)
                 nc.scalar.activation(
-                    scored[:], acc[:, half, :], IDENT, bias=kb_col[:, k : k + 1], scale=ts_col[:, k : k + 1]
+                    scored[:], accs[b][:, half, :], IDENT, bias=cols[:, 8 + k : 9 + k], scale=cols[:, k : k + 1]
                 )
                 nc.tensor.transpose(turned[:, half * P : (half + 1) * P], scored[:], ident[:])
-            best = work.tile([P, N // 32], F32, name="best")
+            best = shared.tile([P, N // 32], F32, name="best%d" % b, offset=SEARCH_BYTES + b * 512)
             nc.vector.tensor_reduce(out=best[:], in_=turned[:].rearrange("p (j s) -> p j s", s=32), axis=X, op=MAX)
             nc.sync.dma_start(out[b], best[:])

@@ -20,7 +20,7 @@ FLOPS = 2 * B * NQ * N * D
 HALVES = N // P
 LIST_COLS = N // 16
 TS_ROW, KB_ROW = 0, 64
-CHUNKS = (((512, 0), (512, 0), (1024, 0)), ((1024, 0), (512, 512), (512, 384)))
+CHUNKS = (((512, 0), (512, 0), (512, 0), (512, 0)), ((1024, 0), (512, 512), (512, 256)))
 WOVEN_ON_VECTOR = 2
 QUERIES_ON_VECTOR = 0
 SEARCH_BYTES = 2048
@@ -66,7 +66,8 @@ def tile_attend_maxsim_tskb_kernel(tc, qT, kT, ts, kb, offs, out):
             q_raws.append(q_raw)
 
         ident = held.tile([P, P], F32, name="ident")
-        make_identity(nc, ident[:])
+        nc.vector.memset(ident[:], 0.0)
+        make_identity(nc, ident[:], nomemset=True)
 
         turned_rows = []
         for name, win, row in (("ts", ts_win, TS_ROW), ("kb", kb_win, KB_ROW)):
@@ -89,8 +90,8 @@ def tile_attend_maxsim_tskb_kernel(tc, qT, kT, ts, kb, offs, out):
                 for lo, hi in ((0, split), (split, width)):
                     if lo == hi:
                         continue
-                    dst = pools[u][:, first + lo : first + hi, :].rearrange("p (c i) e -> p c e i", i=4)
-                    src = raw[:, :, lo:hi].rearrange("p e (c i) -> p c e i", i=4)
+                    dst = pools[u][:, first + lo : first + hi, :]
+                    src = raw[:, :, lo:hi].rearrange("p e w -> p w e")
                     if hi == split:
                         nc.scalar.activation(dst, src, COPY)
                     else:
@@ -116,11 +117,11 @@ def tile_attend_maxsim_tskb_kernel(tc, qT, kT, ts, kb, offs, out):
         for b in range(B):
             flat = grouped[b][:].rearrange("p n t -> p (n t)")
             if b >= WOVEN_ON_VECTOR:
-                dst = flat.bitcast(U32).rearrange("p (c i u) -> p c u i", i=4, u=2)
-                nc.scalar.copy(dst, picked[b][:].rearrange("p u (c i) -> p c u i", i=4))
+                dst = flat.bitcast(U32).rearrange("p (n u) -> p n u", u=2)
+                nc.scalar.copy(dst, picked[b][:].rearrange("p u n -> p n u"))
             else:
-                dst = flat.bitcast(I32).rearrange("p (c i u) -> p c u i", i=4, u=2)
-                nc.vector.tensor_copy(dst, picked[b][:].bitcast(I32).rearrange("p u (c i) -> p c u i", i=4))
+                dst = flat.bitcast(I32).rearrange("p (n u) -> p n u", u=2)
+                nc.vector.tensor_copy(dst, picked[b][:].bitcast(I32).rearrange("p u n -> p n u"))
 
         q_codes, q_scales = [], []
         k_codes, k_scales = [], []

@@ -6,12 +6,15 @@ from concourse.masks import make_identity
 F32 = mybir.dt.float32
 BF16 = mybir.dt.bfloat16
 U32 = mybir.dt.uint32
+I32 = mybir.dt.int32
 U16 = mybir.dt.uint16
 U8 = mybir.dt.uint8
 FP8X4 = mybir.dt.float8_e4m3fn_x4
 COPY = mybir.ActivationFunctionType.Copy
 IDENT = mybir.ActivationFunctionType.Identity
 MAX = mybir.AluOpType.max
+MULT = mybir.AluOpType.mult
+ADD = mybir.AluOpType.add
 X = mybir.AxisListType.X
 
 B, N, T, D, NQ = 4, 256, 2048, 512, 128
@@ -19,19 +22,15 @@ P = 128
 FLOPS = 2 * B * NQ * N * D
 HALVES = N // P
 LIST_COLS = N // 16
-TS_ROW, KB_ROW = 0, 64
+ROW = P - 1
 CHUNKS = (((512, 0), (512, 0), (512, 0), (512, 0)), ((1024, 0), (512, 512), (512, 256)))
-WOVEN_ON_VECTOR = 2
-QUERIES_ON_VECTOR = 0
-SEARCH_BYTES = 2048
-I32 = mybir.dt.int32
+QUERIES_ON_GPSIMD = 3
 
 
 def tile_attend_maxsim_tskb_kernel(tc, qT, kT, ts, kb, offs, out):
     nc = tc.nc
     with ExitStack() as ctx:
         held = ctx.enter_context(tc.tile_pool(name="held", bufs=1))
-        shared = ctx.enter_context(tc.tile_pool(name="shared", bufs=1))
         psum = ctx.enter_context(tc.psum_pool(name="psum", bufs=8))
 
         offsets = held.tile([P, B * LIST_COLS], U16, name="offsets")
@@ -42,8 +41,9 @@ def tile_attend_maxsim_tskb_kernel(tc, qT, kT, ts, kb, offs, out):
 
         ts_win = held.tile([P, T], F32, name="ts_win")
         kb_win = held.tile([P, T], F32, name="kb_win")
-        nc.vector.memset(ts_win[:], 0.0)
-        nc.vector.memset(kb_win[:], 0.0)
+        nc.sync.dma_start(ts_win[ROW:P, :], ts[0:1, :])
+        nc.vector.memset(ts_win[0:ROW, :], 0.0)
+        nc.vector.memset(kb_win[0:ROW, :], 0.0)
 
         k_rows = kT.rearrange("(p u e) w -> p u e w", u=2, e=2)
         chunks = []
@@ -53,16 +53,14 @@ def tile_attend_maxsim_tskb_kernel(tc, qT, kT, ts, kb, offs, out):
                 raw = held.tile([P, 2, width], F32, name="raw%d_%d" % (u, c), tag="raw%d_%d" % (u, c))
                 nc.sync.dma_start(raw[:], k_rows[:, u, :, first : first + width])
                 if (u, c) == (0, 0):
-                    nc.sync.dma_start(ts_win[TS_ROW : TS_ROW + 1, :], ts[0:1, :])
-                if (u, c) == (0, 1):
-                    nc.sync.dma_start(kb_win[KB_ROW : KB_ROW + 1, :], kb[0:1, :])
+                    nc.sync.dma_start(kb_win[ROW:P, :], kb[0:1, :])
                 chunks.append((u, raw, first, width, on_vector))
                 first = first + width
 
         q_raws = []
-        for h in range(2):
-            q_raw = shared.tile([P, 2, 4 * NQ], F32, name="q_raw%d" % h, offset=(2 - 2 * h) * SEARCH_BYTES)
-            nc.sync.dma_start(q_raw[:], qT[2 * h : 2 * h + 2].rearrange("b (p t) q -> p b (t q)", t=4))
+        for b in range(B):
+            q_raw = held.tile([P, 4, NQ], F32, name="q_raw%d" % b)
+            nc.sync.dma_start(q_raw[:], qT[b].rearrange("(p t) q -> p t q", t=4))
             q_raws.append(q_raw)
 
         ident = held.tile([P, P], F32, name="ident")
@@ -70,7 +68,7 @@ def tile_attend_maxsim_tskb_kernel(tc, qT, kT, ts, kb, offs, out):
         make_identity(nc, ident[:], nomemset=True)
 
         turned_rows = []
-        for name, win, row in (("ts", ts_win, TS_ROW), ("kb", kb_win, KB_ROW)):
+        for name, win in (("ts", ts_win), ("kb", kb_win)):
             values = held.tile([P, B * N], F32, name=name + "_picked")
             nc.vector.tensor_copy(values[:], win[:].indirect(offsets[:]))
             for half in range(2):
@@ -78,10 +76,10 @@ def tile_attend_maxsim_tskb_kernel(tc, qT, kT, ts, kb, offs, out):
                 for j in range(4):
                     k = 4 * half + j
                     nc.tensor.transpose(bank[:, j, :], values[:, k * P : (k + 1) * P], ident[:])
-                turned_rows.append(bank[:, :, row])
+                turned_rows.append(bank[:, :, ROW])
 
         pools = [held.tile([P, T, 2], BF16, name="pool%d" % u) for u in range(2)]
-        picked = [shared.tile([P, 2, N], U32, name="picked%d" % b, offset=(B + b) * SEARCH_BYTES) for b in range(B)]
+        picked = [held.tile([P, 2, N], U32, name="picked%d" % b) for b in range(B)]
         for u in range(2):
             for pair, raw, first, width, on_vector in chunks:
                 if pair != u:
@@ -102,59 +100,41 @@ def tile_attend_maxsim_tskb_kernel(tc, qT, kT, ts, kb, offs, out):
         cols = held.tile([P, 16], F32, name="cols", tag="raw1_2")
         for i, turned_row in enumerate(turned_rows):
             nc.scalar.copy(cols[:, 4 * i : 4 * i + 4], turned_row)
-        q_grouped = [held.tile([P, 2, NQ, 4], BF16, name="q_grouped%d" % h, align_bytes=64) for h in range(2)]
-        for b in range(B):
-            dst = q_grouped[b // 2][:, b % 2, :, :].rearrange("p (c i) t -> p c t i", i=4)
-            src = q_raws[b // 2][:, b % 2, :].rearrange("p (t c i) -> p c t i", t=4, i=4)
-            if b < QUERIES_ON_VECTOR:
-                nc.vector.tensor_copy(dst, src)
-            else:
-                nc.scalar.activation(dst, src, COPY)
-        grouped = [held.tile([P, N, 4], BF16, name="grouped%d" % b, align_bytes=64) for b in range(2)] + [
-            shared.tile([P, N, 4], BF16, name="grouped%d" % b, align_bytes=64, offset=(b - 2) * SEARCH_BYTES)
-            for b in range(2, B)
-        ]
-        for b in range(B):
-            flat = grouped[b][:].rearrange("p n t -> p (n t)")
-            if b >= WOVEN_ON_VECTOR:
-                dst = flat.bitcast(U32).rearrange("p (n u) -> p n u", u=2)
-                nc.scalar.copy(dst, picked[b][:].rearrange("p u n -> p n u"))
-            else:
-                dst = flat.bitcast(I32).rearrange("p (n u) -> p n u", u=2)
-                nc.vector.tensor_copy(dst, picked[b][:].bitcast(I32).rearrange("p u n -> p n u"))
 
-        q_codes, q_scales = [], []
-        k_codes, k_scales = [], []
-        for h in range(2):
-            qc = held.tile([P, 2 * NQ], U32, name="q_codes%d" % h, align_bytes=64)
-            qs = held.tile([P, 2 * NQ], U8, name="q_scales%d" % h, align_bytes=64)
-            nc.vector.quantize_mx(
-                out=qc[:].bitcast(FP8X4), scales=qs[:], in_=q_grouped[h][:].rearrange("p b q t -> p (b q t)")
-            )
-            q_codes.append(qc)
-            q_scales.append(qs)
-            for b in (2 * h, 2 * h + 1):
-                kc = held.tile([P, N], U32, name="k_codes%d" % b, align_bytes=64)
-                ks = held.tile([P, N], U8, name="k_scales%d" % b, align_bytes=64)
-                nc.vector.quantize_mx(
-                    out=kc[:].bitcast(FP8X4), scales=ks[:], in_=grouped[b][:].rearrange("p n t -> p (n t)")
-                )
-                k_codes.append(kc)
-                k_scales.append(ks)
+        q_grouped = [held.tile([P, NQ, 4], BF16, name="q_grouped%d" % b, align_bytes=64) for b in range(B)]
+        grouped = [held.tile([P, N, 4], BF16, name="grouped%d" % b, align_bytes=64) for b in range(B)]
+        for b in range(B):
+            if b < QUERIES_ON_GPSIMD:
+                nc.gpsimd.tensor_scalar(q_grouped[b][:], q_raws[b][:].rearrange("p t q -> p q t"), 1.0, 0.0, MULT, ADD)
+            else:
+                dst = q_grouped[b][:].rearrange("p (c i) t -> p c t i", i=4)
+                nc.scalar.activation(dst, q_raws[b][:].rearrange("p t (c i) -> p c t i", i=4), COPY)
+            flat = grouped[b][:].rearrange("p n t -> p (n t)")
+            dst = flat.bitcast(U32).rearrange("p (n u) -> p n u", u=2)
+            nc.scalar.copy(dst, picked[b][:].rearrange("p u n -> p n u"))
 
         accs = []
         for b in range(B):
+            qc = held.tile([P, NQ], U32, name="q_codes%d" % b, align_bytes=64)
+            qs = held.tile([P, NQ], U8, name="q_scales%d" % b, align_bytes=64)
+            nc.vector.quantize_mx(
+                out=qc[:].bitcast(FP8X4), scales=qs[:], in_=q_grouped[b][:].rearrange("p q t -> p (q t)")
+            )
+            kc = held.tile([P, N], U32, name="k_codes%d" % b, align_bytes=64)
+            ks = held.tile([P, N], U8, name="k_scales%d" % b, align_bytes=64)
+            nc.vector.quantize_mx(
+                out=kc[:].bitcast(FP8X4), scales=ks[:], in_=grouped[b][:].rearrange("p n t -> p (n t)")
+            )
             acc = psum.tile([P, HALVES, NQ], F32, name="acc", tag="bank")
             accs.append(acc)
-            q_cols = slice((b % 2) * NQ, (b % 2 + 1) * NQ)
             for half in range(HALVES):
                 s_cols = slice(half * P, (half + 1) * P)
                 nc.tensor.matmul_mx(
                     out=acc[:, half, :],
-                    lhsT=k_codes[b][:, s_cols].bitcast(FP8X4),
-                    lhsT_scale=k_scales[b][:, s_cols],
-                    rhs=q_codes[b // 2][:, q_cols].bitcast(FP8X4),
-                    rhs_scale=q_scales[b // 2][:, q_cols],
+                    lhsT=kc[:, s_cols].bitcast(FP8X4),
+                    lhsT_scale=ks[:, s_cols],
+                    rhs=qc[:].bitcast(FP8X4),
+                    rhs_scale=qs[:],
                     start=True,
                     stop=True,
                 )
@@ -162,11 +142,11 @@ def tile_attend_maxsim_tskb_kernel(tc, qT, kT, ts, kb, offs, out):
             turned = psum.tile([P, N], F32, name="turned", tag="bank")
             for half in range(HALVES):
                 k = HALVES * b + half
-                scored = shared.tile([P, NQ], F32, name="scored%d" % k, offset=(2 * B - 1) * SEARCH_BYTES + k * NQ * 4)
+                scored = held.tile([P, NQ], F32, name="scored%d" % k)
                 nc.scalar.activation(
                     scored[:], accs[b][:, half, :], IDENT, bias=cols[:, 8 + k : 9 + k], scale=cols[:, k : k + 1]
                 )
                 nc.tensor.transpose(turned[:, half * P : (half + 1) * P], scored[:], ident[:])
-            best = shared.tile([P, N // 32], F32, name="best%d" % b, offset=SEARCH_BYTES + b * 512)
+            best = held.tile([P, N // 32], F32, name="best%d" % b)
             nc.vector.tensor_reduce(out=best[:], in_=turned[:].rearrange("p (j s) -> p j s", s=32), axis=X, op=MAX)
             nc.sync.dma_start(out[b], best[:])

@@ -21,17 +21,18 @@ B, N, T, D, NQ = 4, 256, 2048, 512, 128
 P = 128
 FLOPS = 2 * B * NQ * N * D
 HALVES = N // P
+BLOCKS = B * HALVES
 LIST_COLS = N // 16
-ROW = P - 1
+TS_ROW, KB_ROW = 0, 64
 CHUNKS = (((512, 0), (512, 0), (512, 0), (512, 0)), ((1024, 0), (512, 512), (512, 256)))
-QUERIES_ON_GPSIMD = 3
+QUERIES_ON_GPSIMD = 2
 
 
 def tile_attend_maxsim_tskb_kernel(tc, qT, kT, ts, kb, offs, out):
     nc = tc.nc
     with ExitStack() as ctx:
         held = ctx.enter_context(tc.tile_pool(name="held", bufs=1))
-        psum = ctx.enter_context(tc.psum_pool(name="psum", bufs=8))
+        psum = ctx.enter_context(tc.psum_pool(name="psum", bufs=1))
 
         offsets = held.tile([P, B * LIST_COLS], U16, name="offsets")
         nc.sync.dma_start(offsets[:], offs)
@@ -41,9 +42,8 @@ def tile_attend_maxsim_tskb_kernel(tc, qT, kT, ts, kb, offs, out):
 
         ts_win = held.tile([P, T], F32, name="ts_win")
         kb_win = held.tile([P, T], F32, name="kb_win")
-        nc.sync.dma_start(ts_win[ROW:P, :], ts[0:1, :])
-        nc.vector.memset(ts_win[0:ROW, :], 0.0)
-        nc.vector.memset(kb_win[0:ROW, :], 0.0)
+        nc.vector.memset(ts_win[:], 0.0)
+        nc.vector.memset(kb_win[:], 0.0)
 
         k_rows = kT.rearrange("(p u e) w -> p u e w", u=2, e=2)
         chunks = []
@@ -53,13 +53,15 @@ def tile_attend_maxsim_tskb_kernel(tc, qT, kT, ts, kb, offs, out):
                 raw = held.tile([P, 2, width], F32, name="raw%d_%d" % (u, c), tag="raw%d_%d" % (u, c))
                 nc.sync.dma_start(raw[:], k_rows[:, u, :, first : first + width])
                 if (u, c) == (0, 0):
-                    nc.sync.dma_start(kb_win[ROW:P, :], kb[0:1, :])
+                    nc.sync.dma_start(ts_win[TS_ROW : TS_ROW + 1, :], ts[0:1, :])
+                if (u, c) == (0, 1):
+                    nc.sync.dma_start(kb_win[KB_ROW : KB_ROW + 1, :], kb[0:1, :])
                 chunks.append((u, raw, first, width, on_vector))
                 first = first + width
 
         q_raws = []
         for b in range(B):
-            q_raw = held.tile([P, 4, NQ], F32, name="q_raw%d" % b)
+            q_raw = held.tile([P, 4, NQ], F32, name="q_raw%d" % b, tag="q_raw%d" % b)
             nc.sync.dma_start(q_raw[:], qT[b].rearrange("(p t) q -> p t q", t=4))
             q_raws.append(q_raw)
 
@@ -68,17 +70,17 @@ def tile_attend_maxsim_tskb_kernel(tc, qT, kT, ts, kb, offs, out):
         make_identity(nc, ident[:], nomemset=True)
 
         turned_rows = []
-        for name, win in (("ts", ts_win), ("kb", kb_win)):
+        for i, (name, win, row) in enumerate((("ts", ts_win, TS_ROW), ("kb", kb_win, KB_ROW))):
             values = held.tile([P, B * N], F32, name=name + "_picked")
             nc.vector.tensor_copy(values[:], win[:].indirect(offsets[:]))
             for half in range(2):
-                bank = psum.tile([P, 4, P], F32, name="bank", tag="bank")
+                bank = psum.tile([P, 4, P], F32, name="bank", tag="bank%d" % (4 + 2 * i + half))
                 for j in range(4):
                     k = 4 * half + j
                     nc.tensor.transpose(bank[:, j, :], values[:, k * P : (k + 1) * P], ident[:])
-                turned_rows.append(bank[:, :, ROW])
+                turned_rows.append(bank[:, :, row])
 
-        pools = [held.tile([P, T, 2], BF16, name="pool%d" % u) for u in range(2)]
+        pools = [held.tile([P, T, 2], BF16, name="pool%d" % u, tag="pool%d" % u) for u in range(2)]
         picked = [held.tile([P, 2, N], U32, name="picked%d" % b) for b in range(B)]
         for u in range(2):
             for pair, raw, first, width, on_vector in chunks:
@@ -97,40 +99,59 @@ def tile_attend_maxsim_tskb_kernel(tc, qT, kT, ts, kb, offs, out):
             words = pools[u][:].rearrange("p w e -> p (w e)").bitcast(U32)
             for b in range(B):
                 nc.vector.tensor_copy(picked[b][:, u, :], words.indirect(listed(b)))
-        cols = held.tile([P, 16], F32, name="cols", tag="raw1_2")
+        cols = held.tile([P, 2, BLOCKS], F32, name="cols", tag="raw1_%d" % (len(CHUNKS[1]) - 1))
         for i, turned_row in enumerate(turned_rows):
-            nc.scalar.copy(cols[:, 4 * i : 4 * i + 4], turned_row)
+            nc.scalar.copy(cols[:, i // 2, 4 * (i % 2) : 4 * (i % 2) + 4], turned_row)
 
         q_grouped = [held.tile([P, NQ, 4], BF16, name="q_grouped%d" % b, align_bytes=64) for b in range(B)]
-        grouped = [held.tile([P, N, 4], BF16, name="grouped%d" % b, align_bytes=64) for b in range(B)]
+        grouped = [
+            held.tile([P, N, 4], BF16, name="grouped%d" % b, tag="grouped%d" % b, align_bytes=64) for b in range(B - 1)
+        ]
         for b in range(B):
+            dst = q_grouped[b][:].rearrange("p (c i) t -> p c t i", i=4)
+            src = q_raws[b][:].rearrange("p t (c i) -> p c t i", i=4)
             if b < QUERIES_ON_GPSIMD:
                 nc.gpsimd.tensor_scalar(q_grouped[b][:], q_raws[b][:].rearrange("p t q -> p q t"), 1.0, 0.0, MULT, ADD)
             else:
-                dst = q_grouped[b][:].rearrange("p (c i) t -> p c t i", i=4)
-                nc.scalar.activation(dst, q_raws[b][:].rearrange("p t (c i) -> p c t i", i=4), COPY)
-            flat = grouped[b][:].rearrange("p n t -> p (n t)")
-            dst = flat.bitcast(U32).rearrange("p (n u) -> p n u", u=2)
-            nc.scalar.copy(dst, picked[b][:].rearrange("p u n -> p n u"))
+                nc.scalar.activation(dst, src, COPY)
+            if b < B - 1:
+                dst = grouped[b][:].rearrange("p n t -> p (n t)").bitcast(U32).rearrange("p (n u) -> p n u", u=2)
+                nc.scalar.copy(dst, picked[b][:].rearrange("p u n -> p n u"))
 
-        accs = []
-        for b in range(B):
-            qc = held.tile([P, NQ], U32, name="q_codes%d" % b, align_bytes=64)
-            qs = held.tile([P, NQ], U8, name="q_scales%d" % b, align_bytes=64)
+        units = [(b, 0, HALVES) for b in range(B - 1)] + [(B - 1, half, 1) for half in range(HALVES)]
+        q_codes, k_codes = [], []
+        for b, first, count in units:
+            if first == 0:
+                qc = held.tile([P, NQ], U32, name="q_codes%d" % b, align_bytes=64)
+                qs = held.tile([P, NQ], U8, name="q_scales%d" % b, align_bytes=64)
+                nc.vector.quantize_mx(
+                    out=qc[:].bitcast(FP8X4), scales=qs[:], in_=q_grouped[b][:].rearrange("p q t -> p (q t)")
+                )
+                q_codes.append((qc, qs))
+            kc = held.tile([P, count * P], U32, name="k_codes%d_%d" % (b, first), align_bytes=64)
+            ks = held.tile([P, count * P], U8, name="k_scales%d_%d" % (b, first), align_bytes=64)
             nc.vector.quantize_mx(
-                out=qc[:].bitcast(FP8X4), scales=qs[:], in_=q_grouped[b][:].rearrange("p q t -> p (q t)")
+                out=kc[:].bitcast(FP8X4),
+                scales=ks[:],
+                in_=grouped[b][:, first * P : (first + count) * P, :].rearrange("p n t -> p (n t)"),
             )
-            kc = held.tile([P, N], U32, name="k_codes%d" % b, align_bytes=64)
-            ks = held.tile([P, N], U8, name="k_scales%d" % b, align_bytes=64)
-            nc.vector.quantize_mx(
-                out=kc[:].bitcast(FP8X4), scales=ks[:], in_=grouped[b][:].rearrange("p n t -> p (n t)")
-            )
-            acc = psum.tile([P, HALVES, NQ], F32, name="acc", tag="bank")
-            accs.append(acc)
-            for half in range(HALVES):
-                s_cols = slice(half * P, (half + 1) * P)
+            k_codes.append((kc, ks))
+            if b == 0:
+                last = held.tile([P, N, 4], BF16, name="grouped_last", tag="grouped0", align_bytes=64)
+                dst = last[:].rearrange("p n t -> p (n t)").bitcast(I32).rearrange("p (n u) -> p n u", u=2)
+                nc.vector.tensor_copy(dst, picked[B - 1][:].bitcast(I32).rearrange("p u n -> p n u"))
+                grouped.append(last)
+        best = [held.tile([P, N // 32], F32, name="best%d" % b) for b in range(B)]
+
+        def multiply(i, bank):
+            b, first, count = units[i]
+            qc, qs = q_codes[b]
+            kc, ks = k_codes[i]
+            acc = psum.tile([P, count, NQ], F32, name="acc%d" % i, tag="bank%d" % bank)
+            for j in range(count):
+                s_cols = slice(j * P, (j + 1) * P)
                 nc.tensor.matmul_mx(
-                    out=acc[:, half, :],
+                    out=acc[:, j, :],
                     lhsT=kc[:, s_cols].bitcast(FP8X4),
                     lhsT_scale=ks[:, s_cols],
                     rhs=qc[:].bitcast(FP8X4),
@@ -138,15 +159,31 @@ def tile_attend_maxsim_tskb_kernel(tc, qT, kT, ts, kb, offs, out):
                     start=True,
                     stop=True,
                 )
-        for b in range(B):
-            turned = psum.tile([P, N], F32, name="turned", tag="bank")
-            for half in range(HALVES):
-                k = HALVES * b + half
-                scored = held.tile([P, NQ], F32, name="scored%d" % k)
+            return acc
+
+        def finish(i, acc, bank):
+            b, first, count = units[i]
+            turned = psum.tile([P, count * P], F32, name="turned%d" % i, tag="bank%d" % bank)
+            for j in range(count):
+                k = HALVES * b + first + j
+                tag = "q_raw%d" % (B - 1) if k == 0 else "scored%d" % k
+                scored = held.tile([P, NQ], F32, name="scored%d" % k, tag=tag)
                 nc.scalar.activation(
-                    scored[:], accs[b][:, half, :], IDENT, bias=cols[:, 8 + k : 9 + k], scale=cols[:, k : k + 1]
+                    scored[:], acc[:, j, :], IDENT, bias=cols[:, 1, k : k + 1], scale=cols[:, 0, k : k + 1]
                 )
-                nc.tensor.transpose(turned[:, half * P : (half + 1) * P], scored[:], ident[:])
-            best = held.tile([P, N // 32], F32, name="best%d" % b)
-            nc.vector.tensor_reduce(out=best[:], in_=turned[:].rearrange("p (j s) -> p j s", s=32), axis=X, op=MAX)
-            nc.sync.dma_start(out[b], best[:])
+                nc.tensor.transpose(turned[:, j * P : (j + 1) * P], scored[:], ident[:])
+            nc.vector.tensor_reduce(
+                out=best[b][:, 4 * first : 4 * (first + count)],
+                in_=turned[:].rearrange("p (j s) -> p j s", s=32),
+                axis=X,
+                op=MAX,
+            )
+            if first + count == HALVES:
+                nc.sync.dma_start(out[b], best[b][:])
+
+        accs = [multiply(i, i) for i in range(3)]
+        finish(0, accs[0], 4)
+        accs.append(multiply(3, 0))
+        accs.append(multiply(4, 3))
+        for i, bank in ((1, 5), (2, 6), (3, 7), (4, 1)):
+            finish(i, accs[i], bank)

@@ -23,7 +23,7 @@ FLOPS = 2 * B * NQ * N * D
 HALVES = N // P
 BLOCKS = B * HALVES
 LIST_COLS = N // 16
-TS_ROW, KB_ROW = 0, 64
+TS_ROW, KB_ROW = P - 1, 0
 CHUNKS = (((512, 0), (512, 0), (512, 0), (512, 0)), ((1024, 0), (512, 512), (512, 256)))
 QUERIES_ON_GPSIMD = 2
 
@@ -42,8 +42,9 @@ def tile_attend_maxsim_tskb_kernel(tc, qT, kT, ts, kb, offs, out):
 
         ts_win = held.tile([P, T], F32, name="ts_win")
         kb_win = held.tile([P, T], F32, name="kb_win")
-        nc.vector.memset(ts_win[:], 0.0)
+        nc.sync.dma_start(ts_win[TS_ROW:P, :], ts[0:1, :])
         nc.vector.memset(kb_win[:], 0.0)
+        nc.vector.memset(ts_win[0:TS_ROW, :], 0.0)
 
         k_rows = kT.rearrange("(p u e) w -> p u e w", u=2, e=2)
         chunks = []
@@ -52,8 +53,6 @@ def tile_attend_maxsim_tskb_kernel(tc, qT, kT, ts, kb, offs, out):
             for c, (width, on_vector) in enumerate(CHUNKS[u]):
                 raw = held.tile([P, 2, width], F32, name="raw%d_%d" % (u, c), tag="raw%d_%d" % (u, c))
                 nc.sync.dma_start(raw[:], k_rows[:, u, :, first : first + width])
-                if (u, c) == (0, 0):
-                    nc.sync.dma_start(ts_win[TS_ROW : TS_ROW + 1, :], ts[0:1, :])
                 if (u, c) == (0, 1):
                     nc.sync.dma_start(kb_win[KB_ROW : KB_ROW + 1, :], kb[0:1, :])
                 chunks.append((u, raw, first, width, on_vector))
@@ -118,7 +117,7 @@ def tile_attend_maxsim_tskb_kernel(tc, qT, kT, ts, kb, offs, out):
                 dst = grouped[b][:].rearrange("p n t -> p (n t)").bitcast(U32).rearrange("p (n u) -> p n u", u=2)
                 nc.scalar.copy(dst, picked[b][:].rearrange("p u n -> p n u"))
 
-        units = [(b, 0, HALVES) for b in range(B - 1)] + [(B - 1, half, 1) for half in range(HALVES)]
+        units = [(b, 0, HALVES) for b in range(B)]
         q_codes, k_codes = [], []
         for b, first, count in units:
             if first == 0:
@@ -168,9 +167,11 @@ def tile_attend_maxsim_tskb_kernel(tc, qT, kT, ts, kb, offs, out):
                 k = HALVES * b + first + j
                 tag = "q_raw%d" % (B - 1) if k == 0 else "scored%d" % k
                 scored = held.tile([P, NQ], F32, name="scored%d" % k, tag=tag)
-                nc.scalar.activation(
-                    scored[:], acc[:, j, :], IDENT, bias=cols[:, 1, k : k + 1], scale=cols[:, 0, k : k + 1]
-                )
+                scale, bias = cols[:, 0, k : k + 1], cols[:, 1, k : k + 1]
+                if b == B - 1:
+                    nc.vector.tensor_scalar(scored[:], acc[:, j, :], scale, bias, MULT, ADD)
+                else:
+                    nc.scalar.activation(scored[:], acc[:, j, :], IDENT, bias=bias, scale=scale)
                 nc.tensor.transpose(turned[:, j * P : (j + 1) * P], scored[:], ident[:])
             nc.vector.tensor_reduce(
                 out=best[b][:, 4 * first : 4 * (first + count)],
@@ -181,9 +182,6 @@ def tile_attend_maxsim_tskb_kernel(tc, qT, kT, ts, kb, offs, out):
             if first + count == HALVES:
                 nc.sync.dma_start(out[b], best[b][:])
 
-        accs = [multiply(i, i) for i in range(3)]
-        finish(0, accs[0], 4)
-        accs.append(multiply(3, 0))
-        accs.append(multiply(4, 3))
-        for i, bank in ((1, 5), (2, 6), (3, 7), (4, 1)):
-            finish(i, accs[i], bank)
+        accs = [multiply(i, i) for i in range(B)]
+        for i in range(B):
+            finish(i, accs[i], B + i)

@@ -23,8 +23,9 @@ FLOPS = 2 * B * NQ * N * D
 HALVES = N // P
 BLOCKS = B * HALVES
 LIST_COLS = N // 16
-TS_ROW, KB_ROW = P - 1, 0
-CHUNKS = (((512, 0), (512, 0), (512, 0), (512, 0)), ((1024, 0), (512, 512), (512, 256)))
+ROW = P - 1
+ZERO_PIECES = 4
+CHUNKS = (((512, 0), (512, 0), (512, 0), (512, 512)), ((512, 0), (512, 0), (512, 256), (384, 256), (128, 128)))
 QUERIES_ON_GPSIMD = 2
 
 
@@ -42,9 +43,10 @@ def tile_attend_maxsim_tskb_kernel(tc, qT, kT, ts, kb, offs, out):
 
         ts_win = held.tile([P, T], F32, name="ts_win")
         kb_win = held.tile([P, T], F32, name="kb_win")
-        nc.sync.dma_start(ts_win[TS_ROW:P, :], ts[0:1, :])
-        nc.vector.memset(kb_win[:], 0.0)
-        nc.vector.memset(ts_win[0:TS_ROW, :], 0.0)
+        nc.sync.dma_start(ts_win[ROW:P, :], ts[0:1, :])
+        nc.vector.memset(ts_win[0:ROW, :], 0.0)
+        for piece in range(ZERO_PIECES):
+            nc.gpsimd.memset(kb_win[0:ROW, piece * T // ZERO_PIECES : (piece + 1) * T // ZERO_PIECES], 0.0)
 
         k_rows = kT.rearrange("(p u e) w -> p u e w", u=2, e=2)
         chunks = []
@@ -53,8 +55,8 @@ def tile_attend_maxsim_tskb_kernel(tc, qT, kT, ts, kb, offs, out):
             for c, (width, on_vector) in enumerate(CHUNKS[u]):
                 raw = held.tile([P, 2, width], F32, name="raw%d_%d" % (u, c), tag="raw%d_%d" % (u, c))
                 nc.sync.dma_start(raw[:], k_rows[:, u, :, first : first + width])
-                if (u, c) == (0, 1):
-                    nc.sync.dma_start(kb_win[KB_ROW : KB_ROW + 1, :], kb[0:1, :])
+                if (u, c) == (0, 0):
+                    nc.sync.dma_start(kb_win[ROW:P, :], kb[0:1, :])
                 chunks.append((u, raw, first, width, on_vector))
                 first = first + width
 
@@ -69,7 +71,7 @@ def tile_attend_maxsim_tskb_kernel(tc, qT, kT, ts, kb, offs, out):
         make_identity(nc, ident[:], nomemset=True)
 
         turned_rows = []
-        for i, (name, win, row) in enumerate((("ts", ts_win, TS_ROW), ("kb", kb_win, KB_ROW))):
+        for i, (name, win) in enumerate((("ts", ts_win), ("kb", kb_win))):
             values = held.tile([P, B * N], F32, name=name + "_picked")
             nc.vector.tensor_copy(values[:], win[:].indirect(offsets[:]))
             for half in range(2):
@@ -77,7 +79,7 @@ def tile_attend_maxsim_tskb_kernel(tc, qT, kT, ts, kb, offs, out):
                 for j in range(4):
                     k = 4 * half + j
                     nc.tensor.transpose(bank[:, j, :], values[:, k * P : (k + 1) * P], ident[:])
-                turned_rows.append(bank[:, :, row])
+                turned_rows.append(bank[:, :, ROW])
 
         pools = [held.tile([P, T, 2], BF16, name="pool%d" % u, tag="pool%d" % u) for u in range(2)]
         picked = [held.tile([P, 2, N], U32, name="picked%d" % b) for b in range(B)]

@@ -18,15 +18,21 @@ ADD = mybir.AluOpType.add
 X = mybir.AxisListType.X
 
 B, N, T, D, NQ = 4, 256, 2048, 512, 128
+PASSAGE = 32
 P = 128
+PACK = 4
 FLOPS = 2 * B * NQ * N * D
 HALVES = N // P
-BLOCKS = B * HALVES
 LIST_COLS = N // 16
+PER_BANK = 4
+
 ROW = P - 1
 ZERO_PIECES = 4
-CHUNKS = (((512, 0), (512, 0), (512, 0), (512, 512)), ((512, 0), (512, 0), (512, 256), (384, 256), (128, 128)))
-QUERIES_ON_GPSIMD = 2
+
+CHUNKS = (((512, 0), (512, 0), (512, 0), (512, 192)), ((512, 0), (512, 0), (512, 256), (384, 192), (128, 64)))
+QUERIES_ON_GPSIMD = (128, 128, 48, 0)
+SLOTS_ON_VECTOR = (0, 0, 128, 0)
+RUNS = ((("k", 0), ("q", 0), ("q", 1)), (("k", 1),), (("k", 2),), (("q", 2),), (("k", 3),), (("q", 3),))
 
 
 def tile_attend_maxsim_tskb_kernel(tc, qT, kT, ts, kb, offs, out):
@@ -38,9 +44,6 @@ def tile_attend_maxsim_tskb_kernel(tc, qT, kT, ts, kb, offs, out):
         offsets = held.tile([P, B * LIST_COLS], U16, name="offsets")
         nc.sync.dma_start(offsets[:], offs)
 
-        def listed(b):
-            return offsets[:, b * LIST_COLS : (b + 1) * LIST_COLS]
-
         ts_win = held.tile([P, T], F32, name="ts_win")
         kb_win = held.tile([P, T], F32, name="kb_win")
         nc.sync.dma_start(ts_win[ROW:P, :], ts[0:1, :])
@@ -49,7 +52,7 @@ def tile_attend_maxsim_tskb_kernel(tc, qT, kT, ts, kb, offs, out):
             nc.gpsimd.memset(kb_win[0:ROW, piece * T // ZERO_PIECES : (piece + 1) * T // ZERO_PIECES], 0.0)
 
         k_rows = kT.rearrange("(p u e) w -> p u e w", u=2, e=2)
-        chunks = []
+        loaded = ([], [])
         for u in range(2):
             first = 0
             for c, (width, on_vector) in enumerate(CHUNKS[u]):
@@ -57,13 +60,12 @@ def tile_attend_maxsim_tskb_kernel(tc, qT, kT, ts, kb, offs, out):
                 nc.sync.dma_start(raw[:], k_rows[:, u, :, first : first + width])
                 if (u, c) == (0, 0):
                     nc.sync.dma_start(kb_win[ROW:P, :], kb[0:1, :])
-                chunks.append((u, raw, first, width, on_vector))
+                loaded[u].append((raw, first, width, on_vector))
                 first = first + width
-
         q_raws = []
         for b in range(B):
-            q_raw = held.tile([P, 4, NQ], F32, name="q_raw%d" % b, tag="q_raw%d" % b)
-            nc.sync.dma_start(q_raw[:], qT[b].rearrange("(p t) q -> p t q", t=4))
+            q_raw = held.tile([P, PACK, NQ], F32, name="q_raw%d" % b, tag="q_raw%d" % b)
+            nc.sync.dma_start(q_raw[:], qT[b].rearrange("(p t) q -> p t q", t=PACK))
             q_raws.append(q_raw)
 
         ident = held.tile([P, P], F32, name="ident")
@@ -74,116 +76,109 @@ def tile_attend_maxsim_tskb_kernel(tc, qT, kT, ts, kb, offs, out):
         for i, (name, win) in enumerate((("ts", ts_win), ("kb", kb_win))):
             values = held.tile([P, B * N], F32, name=name + "_picked")
             nc.vector.tensor_copy(values[:], win[:].indirect(offsets[:]))
-            for half in range(2):
-                bank = psum.tile([P, 4, P], F32, name="bank", tag="bank%d" % (4 + 2 * i + half))
-                for j in range(4):
-                    k = 4 * half + j
-                    nc.tensor.transpose(bank[:, j, :], values[:, k * P : (k + 1) * P], ident[:])
+            for part in range(2):
+                bank = psum.tile([P, PER_BANK, P], F32, name="bank", tag="bank%d" % (B + 2 * i + part))
+                for j in range(PER_BANK):
+                    block = PER_BANK * part + j
+                    nc.tensor.transpose(bank[:, j, :], values[:, block * P : (block + 1) * P], ident[:])
                 turned_rows.append(bank[:, :, ROW])
 
-        pools = [held.tile([P, T, 2], BF16, name="pool%d" % u, tag="pool%d" % u) for u in range(2)]
+        pairs = [held.tile([P, T, 2], BF16, name="pair%d" % u) for u in range(2)]
         picked = [held.tile([P, 2, N], U32, name="picked%d" % b) for b in range(B)]
         for u in range(2):
-            for pair, raw, first, width, on_vector in chunks:
-                if pair != u:
-                    continue
+            for raw, first, width, on_vector in loaded[u]:
                 split = width - on_vector
-                for lo, hi in ((0, split), (split, width)):
-                    if lo == hi:
-                        continue
-                    dst = pools[u][:, first + lo : first + hi, :]
-                    src = raw[:, :, lo:hi].rearrange("p e w -> p w e")
-                    if hi == split:
-                        nc.scalar.activation(dst, src, COPY)
-                    else:
-                        nc.vector.tensor_copy(dst, src)
-            words = pools[u][:].rearrange("p w e -> p (w e)").bitcast(U32)
-            for b in range(B):
-                nc.vector.tensor_copy(picked[b][:, u, :], words.indirect(listed(b)))
-        cols = held.tile([P, 2, BLOCKS], F32, name="cols", tag="raw1_%d" % (len(CHUNKS[1]) - 1))
-        for i, turned_row in enumerate(turned_rows):
-            nc.scalar.copy(cols[:, i // 2, 4 * (i % 2) : 4 * (i % 2) + 4], turned_row)
-
-        q_grouped = [held.tile([P, NQ, 4], BF16, name="q_grouped%d" % b, align_bytes=64) for b in range(B)]
-        grouped = [
-            held.tile([P, N, 4], BF16, name="grouped%d" % b, tag="grouped%d" % b, align_bytes=64) for b in range(B - 1)
-        ]
-        for b in range(B):
-            dst = q_grouped[b][:].rearrange("p (c i) t -> p c t i", i=4)
-            src = q_raws[b][:].rearrange("p t (c i) -> p c t i", i=4)
-            if b < QUERIES_ON_GPSIMD:
-                nc.gpsimd.tensor_scalar(q_grouped[b][:], q_raws[b][:].rearrange("p t q -> p q t"), 1.0, 0.0, MULT, ADD)
-            else:
-                nc.scalar.activation(dst, src, COPY)
-            if b < B - 1:
-                dst = grouped[b][:].rearrange("p n t -> p (n t)").bitcast(U32).rearrange("p (n u) -> p n u", u=2)
-                nc.scalar.copy(dst, picked[b][:].rearrange("p u n -> p n u"))
-
-        units = [(b, 0, HALVES) for b in range(B)]
-        q_codes, k_codes = [], []
-        for b, first, count in units:
-            if first == 0:
-                qc = held.tile([P, NQ], U32, name="q_codes%d" % b, align_bytes=64)
-                qs = held.tile([P, NQ], U8, name="q_scales%d" % b, align_bytes=64)
-                nc.vector.quantize_mx(
-                    out=qc[:].bitcast(FP8X4), scales=qs[:], in_=q_grouped[b][:].rearrange("p q t -> p (q t)")
+                nc.scalar.activation(
+                    pairs[u][:, first : first + split, :], raw[:, :, 0:split].rearrange("p e w -> p w e"), COPY
                 )
-                q_codes.append((qc, qs))
-            kc = held.tile([P, count * P], U32, name="k_codes%d_%d" % (b, first), align_bytes=64)
-            ks = held.tile([P, count * P], U8, name="k_scales%d_%d" % (b, first), align_bytes=64)
-            nc.vector.quantize_mx(
-                out=kc[:].bitcast(FP8X4),
-                scales=ks[:],
-                in_=grouped[b][:, first * P : (first + count) * P, :].rearrange("p n t -> p (n t)"),
-            )
-            k_codes.append((kc, ks))
-            if b == 0:
-                last = held.tile([P, N, 4], BF16, name="grouped_last", tag="grouped0", align_bytes=64)
-                dst = last[:].rearrange("p n t -> p (n t)").bitcast(I32).rearrange("p (n u) -> p n u", u=2)
-                nc.vector.tensor_copy(dst, picked[B - 1][:].bitcast(I32).rearrange("p u n -> p n u"))
-                grouped.append(last)
-        best = [held.tile([P, N // 32], F32, name="best%d" % b) for b in range(B)]
+                if on_vector > 0:
+                    nc.vector.tensor_copy(
+                        pairs[u][:, first + split : first + width, :],
+                        raw[:, :, split:width].rearrange("p e w -> p w e"),
+                    )
+            words = pairs[u][:].rearrange("p w e -> p (w e)").bitcast(U32)
+            for b in range(B):
+                listed = offsets[:, b * LIST_COLS : (b + 1) * LIST_COLS]
+                nc.vector.tensor_copy(picked[b][:, u, :], words.indirect(listed))
 
-        def multiply(i, bank):
-            b, first, count = units[i]
-            qc, qs = q_codes[b]
-            kc, ks = k_codes[i]
-            acc = psum.tile([P, count, NQ], F32, name="acc%d" % i, tag="bank%d" % bank)
-            for j in range(count):
-                s_cols = slice(j * P, (j + 1) * P)
+        cols = held.tile([P, 2, B * HALVES], F32, name="cols", tag="raw1_%d" % (len(CHUNKS[1]) - 1))
+        for i, turned_row in enumerate(turned_rows):
+            nc.scalar.copy(cols[:, i // 2, PER_BANK * (i % 2) : PER_BANK * (i % 2 + 1)], turned_row)
+
+        def weave_keys(b, woven):
+            flat = woven.rearrange("p n t -> p (n t)")
+            split = N - SLOTS_ON_VECTOR[b]
+            dst = flat.bitcast(U32).rearrange("p (n u) -> p n u", u=2)
+            nc.scalar.copy(dst[:, 0:split, :], picked[b][:, :, 0:split].rearrange("p u n -> p n u"))
+            if split < N:
+                dst = flat.bitcast(I32).rearrange("p (n u) -> p n u", u=2)
+                nc.vector.tensor_copy(
+                    dst[:, split:N, :], picked[b][:].bitcast(I32)[:, :, split:N].rearrange("p u n -> p n u")
+                )
+
+        def weave_queries(b, woven):
+            split = QUERIES_ON_GPSIMD[b]
+            if split > 0:
+                src = q_raws[b][:, :, 0:split].rearrange("p t q -> p q t")
+                nc.gpsimd.tensor_scalar(woven[:, 0:split, :], src, 1.0, 0.0, MULT, ADD)
+            if split < NQ:
+                nc.scalar.activation(
+                    woven[:, split:NQ, :].rearrange("p (c i) t -> p c t i", i=4),
+                    q_raws[b][:, :, split:NQ].rearrange("p t (c i) -> p c t i", i=4),
+                    COPY,
+                )
+
+        operands = {}
+        for r, run in enumerate(RUNS):
+            widths = [N if kind == "k" else NQ for kind, b in run]
+            woven = held.tile([P, sum(widths), PACK], BF16, name="woven%d" % r, align_bytes=64)
+            codes = held.tile([P, sum(widths)], U32, name="codes%d" % r, align_bytes=64)
+            scales = held.tile([P, sum(widths)], U8, name="scales%d" % r, align_bytes=64)
+            first = 0
+            for (kind, b), width in zip(run, widths):
+                cut = slice(first, first + width)
+                if kind == "k":
+                    weave_keys(b, woven[:, cut, :])
+                else:
+                    weave_queries(b, woven[:, cut, :])
+                operands[(kind, b)] = (codes[:, cut], scales[:, cut])
+                first = first + width
+            nc.vector.quantize_mx(
+                out=codes[:].bitcast(FP8X4), scales=scales[:], in_=woven[:].rearrange("p n t -> p (n t)")
+            )
+
+        sums = []
+        for b in range(B):
+            q_codes, q_scales = operands[("q", b)]
+            k_codes, k_scales = operands[("k", b)]
+            acc = psum.tile([P, HALVES, NQ], F32, name="acc%d" % b, tag="bank%d" % b)
+            for half in range(HALVES):
+                slots = slice(half * P, (half + 1) * P)
                 nc.tensor.matmul_mx(
-                    out=acc[:, j, :],
-                    lhsT=kc[:, s_cols].bitcast(FP8X4),
-                    lhsT_scale=ks[:, s_cols],
-                    rhs=qc[:].bitcast(FP8X4),
-                    rhs_scale=qs[:],
+                    out=acc[:, half, :],
+                    lhsT=k_codes[:, slots].bitcast(FP8X4),
+                    lhsT_scale=k_scales[:, slots],
+                    rhs=q_codes.bitcast(FP8X4),
+                    rhs_scale=q_scales,
                     start=True,
                     stop=True,
                 )
-            return acc
+            sums.append(acc)
 
-        def finish(i, acc, bank):
-            b, first, count = units[i]
-            turned = psum.tile([P, count * P], F32, name="turned%d" % i, tag="bank%d" % bank)
-            for j in range(count):
-                k = HALVES * b + first + j
-                tag = "q_raw%d" % (B - 1) if k == 0 else "scored%d" % k
-                scored = held.tile([P, NQ], F32, name="scored%d" % k, tag=tag)
-                scale, bias = cols[:, 0, k : k + 1], cols[:, 1, k : k + 1]
+        for b in range(B):
+            turned = psum.tile([P, N], F32, name="turned%d" % b, tag="bank%d" % (B + b))
+            for half in range(HALVES):
+                block = HALVES * b + half
+                tag = "q_raw%d" % (B - 1) if block == 0 else "scored%d" % block
+                scored = held.tile([P, NQ], F32, name="scored%d" % block, tag=tag)
+                scale, bias = cols[:, 0, block : block + 1], cols[:, 1, block : block + 1]
                 if b == B - 1:
-                    nc.vector.tensor_scalar(scored[:], acc[:, j, :], scale, bias, MULT, ADD)
+                    nc.vector.tensor_scalar(scored[:], sums[b][:, half, :], scale, bias, MULT, ADD)
                 else:
-                    nc.scalar.activation(scored[:], acc[:, j, :], IDENT, bias=bias, scale=scale)
-                nc.tensor.transpose(turned[:, j * P : (j + 1) * P], scored[:], ident[:])
+                    nc.scalar.activation(scored[:], sums[b][:, half, :], IDENT, bias=bias, scale=scale)
+                nc.tensor.transpose(turned[:, half * P : (half + 1) * P], scored[:], ident[:])
+            best = held.tile([P, N // PASSAGE], F32, name="best%d" % b)
             nc.vector.tensor_reduce(
-                out=best[b][:, 4 * first : 4 * (first + count)],
-                in_=turned[:].rearrange("p (j s) -> p j s", s=32),
-                axis=X,
-                op=MAX,
+                out=best[:], in_=turned[:].rearrange("p (j s) -> p j s", s=PASSAGE), axis=X, op=MAX
             )
-            if first + count == HALVES:
-                nc.sync.dma_start(out[b], best[b][:])
-
-        accs = [multiply(i, i) for i in range(B)]
-        for i in range(B):
-            finish(i, accs[i], B + i)
+            nc.sync.dma_start(out[b], best[:])

@@ -15,7 +15,7 @@ IDENT = mybir.ActivationFunctionType.Identity
 MAX = mybir.AluOpType.max
 MULT = mybir.AluOpType.mult
 ADD = mybir.AluOpType.add
-X = mybir.AxisListType.X
+XY = mybir.AxisListType.XY
 
 B, N, T, D, NQ = 4, 256, 2048, 512, 128
 PASSAGE = 32
@@ -29,10 +29,11 @@ PER_BANK = 4
 ROW = P - 1
 ZERO_PIECES = 4
 
-CHUNKS = (((512, 0), (512, 0), (512, 0), (512, 192)), ((512, 0), (512, 0), (512, 256), (384, 192), (128, 64)))
-QUERIES_ON_GPSIMD = (128, 128, 48, 0)
-SLOTS_ON_VECTOR = (0, 0, 128, 0)
-RUNS = ((("k", 0), ("q", 0), ("q", 1)), (("k", 1),), (("k", 2),), (("q", 2),), (("k", 3),), (("q", 3),))
+CHUNKS = (640, 640, 384, 256, 128)
+QUERIES_ON_GPSIMD = (128, 128, 128, 0)
+QUAD = 4
+SIDE_BY_SIDE = (("k", 0), ("q", 0), ("q", 1), ("k", 1), ("q", 2), ("k", 2), ("k", 3), ("q", 3))
+RUN = 512
 
 
 def tile_attend_maxsim_tskb_kernel(tc, qT, kT, ts, kb, offs, out):
@@ -46,22 +47,20 @@ def tile_attend_maxsim_tskb_kernel(tc, qT, kT, ts, kb, offs, out):
 
         ts_win = held.tile([P, T], F32, name="ts_win")
         kb_win = held.tile([P, T], F32, name="kb_win")
-        nc.sync.dma_start(ts_win[ROW:P, :], ts[0:1, :])
+        nc.scalar.dma_start(ts_win[ROW:P, :], ts[0:1, :])
+        nc.scalar.dma_start(kb_win[ROW:P, :], kb[0:1, :])
         nc.vector.memset(ts_win[0:ROW, :], 0.0)
         for piece in range(ZERO_PIECES):
             nc.gpsimd.memset(kb_win[0:ROW, piece * T // ZERO_PIECES : (piece + 1) * T // ZERO_PIECES], 0.0)
 
-        k_rows = kT.rearrange("(p u e) w -> p u e w", u=2, e=2)
-        loaded = ([], [])
-        for u in range(2):
-            first = 0
-            for c, (width, on_vector) in enumerate(CHUNKS[u]):
-                raw = held.tile([P, 2, width], F32, name="raw%d_%d" % (u, c), tag="raw%d_%d" % (u, c))
-                nc.sync.dma_start(raw[:], k_rows[:, u, :, first : first + width])
-                if (u, c) == (0, 0):
-                    nc.sync.dma_start(kb_win[ROW:P, :], kb[0:1, :])
-                loaded[u].append((raw, first, width, on_vector))
-                first = first + width
+        k_rows = kT.rearrange("(p t) w -> p t w", t=PACK)
+        loaded = []
+        first = 0
+        for c, width in enumerate(CHUNKS):
+            raw = held.tile([P, PACK, width], F32, name="raw%d" % c, tag="raw%d" % c)
+            nc.sync.dma_start(raw[:], k_rows[:, :, first : first + width])
+            loaded.append((raw, first, width))
+            first = first + width
         q_raws = []
         for b in range(B):
             q_raw = held.tile([P, PACK, NQ], F32, name="q_raw%d" % b, tag="q_raw%d" % b)
@@ -75,7 +74,10 @@ def tile_attend_maxsim_tskb_kernel(tc, qT, kT, ts, kb, offs, out):
         turned_rows = []
         for i, (name, win) in enumerate((("ts", ts_win), ("kb", kb_win))):
             values = held.tile([P, B * N], F32, name=name + "_picked")
-            nc.vector.tensor_copy(values[:], win[:].indirect(offsets[:]))
+            nc.vector.tensor_copy(
+                values[:].bitcast(U32).rearrange("p (b x m i) -> p b m x i", b=B, x=4, i=QUAD),
+                win[:].bitcast(U32).indirect(offsets[:]),
+            )
             for part in range(2):
                 bank = psum.tile([P, PER_BANK, P], F32, name="bank", tag="bank%d" % (B + 2 * i + part))
                 for j in range(PER_BANK):
@@ -83,37 +85,34 @@ def tile_attend_maxsim_tskb_kernel(tc, qT, kT, ts, kb, offs, out):
                     nc.tensor.transpose(bank[:, j, :], values[:, block * P : (block + 1) * P], ident[:])
                 turned_rows.append(bank[:, :, ROW])
 
-        pairs = [held.tile([P, T, 2], BF16, name="pair%d" % u) for u in range(2)]
-        picked = [held.tile([P, 2, N], U32, name="picked%d" % b) for b in range(B)]
-        for u in range(2):
-            for raw, first, width, on_vector in loaded[u]:
-                split = width - on_vector
-                nc.scalar.activation(
-                    pairs[u][:, first : first + split, :], raw[:, :, 0:split].rearrange("p e w -> p w e"), COPY
-                )
-                if on_vector > 0:
-                    nc.vector.tensor_copy(
-                        pairs[u][:, first + split : first + width, :],
-                        raw[:, :, split:width].rearrange("p e w -> p w e"),
-                    )
-            words = pairs[u][:].rearrange("p w e -> p (w e)").bitcast(U32)
-            for b in range(B):
-                listed = offsets[:, b * LIST_COLS : (b + 1) * LIST_COLS]
-                nc.vector.tensor_copy(picked[b][:, u, :], words.indirect(listed))
-
-        cols = held.tile([P, 2, B * HALVES], F32, name="cols", tag="raw1_%d" % (len(CHUNKS[1]) - 1))
-        for i, turned_row in enumerate(turned_rows):
-            nc.scalar.copy(cols[:, i // 2, PER_BANK * (i % 2) : PER_BANK * (i % 2 + 1)], turned_row)
-
-        def weave_keys(b, woven):
-            flat = woven.rearrange("p n t -> p (n t)")
-            split = N - SLOTS_ON_VECTOR[b]
-            dst = flat.bitcast(U32).rearrange("p (n u) -> p n u", u=2)
-            nc.scalar.copy(dst[:, 0:split, :], picked[b][:, :, 0:split].rearrange("p u n -> p n u"))
-            if split < N:
-                dst = flat.bitcast(I32).rearrange("p (n u) -> p n u", u=2)
+        words = held.tile([P, T // 2, PACK], BF16, name="words")
+        halves = [held.tile([P, T // 4, PACK], BF16, name="halves%d" % h) for h in range(2)]
+        for raw, first, width in loaded:
+            nc.scalar.activation(
+                words[:, first // 2 : (first + width) // 2, :].rearrange("p (m i) t -> p m t i", i=QUAD),
+                raw[:].rearrange("p t (m a i) -> p a m t i", a=2, i=QUAD)[:, 0],
+                COPY,
+            )
+            for h in range(2):
                 nc.vector.tensor_copy(
-                    dst[:, split:N, :], picked[b][:].bitcast(I32)[:, :, split:N].rearrange("p u n -> p n u")
+                    halves[h][:, first // 4 : (first + width) // 4, :].rearrange("p (m i) t -> p m t i", i=QUAD),
+                    raw[:].rearrange("p t (m h a i) -> p h a m t i", h=2, a=2, i=QUAD)[:, h, 1],
+                )
+
+        cols = held.tile([P, 2, B * HALVES], F32, name="cols", tag="raw%d" % (len(CHUNKS) - 3))
+        for i, turned_row in enumerate(turned_rows):
+            nc.vector.tensor_copy(cols[:, i // 2, PER_BANK * (i % 2) : PER_BANK * (i % 2 + 1)], turned_row)
+
+        def gather_keys(b, woven):
+            listed = offsets[:, b * LIST_COLS : (b + 1) * LIST_COLS]
+            flat = woven.rearrange("p n t -> p (n t)")
+            dst = flat.bitcast(U32).rearrange("p (h a m w) -> p a m h w", h=2, a=2, w=2 * QUAD)
+            nc.vector.tensor_copy(dst[:, 0], words[:].rearrange("p n t -> p (n t)").bitcast(U32).indirect(listed))
+            for h in range(2):
+                nc.scalar.activation(
+                    flat[:, (2 * h + 1) * N : (2 * h + 2) * N],
+                    halves[h][:].rearrange("p n t -> p (n t)").indirect(listed),
+                    COPY,
                 )
 
         def weave_queries(b, woven):
@@ -128,24 +127,28 @@ def tile_attend_maxsim_tskb_kernel(tc, qT, kT, ts, kb, offs, out):
                     COPY,
                 )
 
-        operands = {}
-        for r, run in enumerate(RUNS):
-            widths = [N if kind == "k" else NQ for kind, b in run]
-            woven = held.tile([P, sum(widths), PACK], BF16, name="woven%d" % r, align_bytes=64)
-            codes = held.tile([P, sum(widths)], U32, name="codes%d" % r, align_bytes=64)
-            scales = held.tile([P, sum(widths)], U8, name="scales%d" % r, align_bytes=64)
-            first = 0
-            for (kind, b), width in zip(run, widths):
-                cut = slice(first, first + width)
-                if kind == "k":
-                    weave_keys(b, woven[:, cut, :])
-                else:
-                    weave_queries(b, woven[:, cut, :])
-                operands[(kind, b)] = (codes[:, cut], scales[:, cut])
-                first = first + width
+        columns = B * (N + NQ)
+        woven = held.tile([P, columns, PACK], BF16, name="woven", tag="woven", align_bytes=64)
+        codes = held.tile([P, columns], U32, name="codes", align_bytes=64)
+        scales = held.tile([P, columns], U8, name="scales", align_bytes=64)
+        place = {}
+        first = 0
+        for kind, b in SIDE_BY_SIDE:
+            width = N if kind == "k" else NQ
+            place[(kind, b)] = slice(first, first + width)
+            first = first + width
+        for b in range(B):
+            gather_keys(b, woven[:, place[("k", b)], :])
+        for b in range(B):
+            weave_queries(b, woven[:, place[("q", b)], :])
+        for first in range(0, columns, RUN):
+            cut = slice(first, first + RUN)
             nc.vector.quantize_mx(
-                out=codes[:].bitcast(FP8X4), scales=scales[:], in_=woven[:].rearrange("p n t -> p (n t)")
+                out=codes[:, cut].bitcast(FP8X4),
+                scales=scales[:, cut],
+                in_=woven[:, cut, :].rearrange("p n t -> p (n t)"),
             )
+        operands = {member: (codes[:, cut], scales[:, cut]) for member, cut in place.items()}
 
         sums = []
         for b in range(B):
@@ -165,20 +168,20 @@ def tile_attend_maxsim_tskb_kernel(tc, qT, kT, ts, kb, offs, out):
                 )
             sums.append(acc)
 
+        scored_all = held.tile([P, B * HALVES, NQ], F32, name="scored", tag="woven", align_bytes=64)
         for b in range(B):
             turned = psum.tile([P, N], F32, name="turned%d" % b, tag="bank%d" % (B + b))
             for half in range(HALVES):
                 block = HALVES * b + half
-                tag = "q_raw%d" % (B - 1) if block == 0 else "scored%d" % block
-                scored = held.tile([P, NQ], F32, name="scored%d" % block, tag=tag)
+                scored = scored_all[:, block, :]
                 scale, bias = cols[:, 0, block : block + 1], cols[:, 1, block : block + 1]
                 if b == B - 1:
-                    nc.vector.tensor_scalar(scored[:], sums[b][:, half, :], scale, bias, MULT, ADD)
+                    nc.vector.tensor_scalar(scored, sums[b][:, half, :], scale, bias, MULT, ADD)
                 else:
-                    nc.scalar.activation(scored[:], sums[b][:, half, :], IDENT, bias=bias, scale=scale)
-                nc.tensor.transpose(turned[:, half * P : (half + 1) * P], scored[:], ident[:])
+                    nc.scalar.activation(scored, sums[b][:, half, :], IDENT, bias=bias, scale=scale)
+                nc.tensor.transpose(turned[:, half * P : (half + 1) * P], scored, ident[:])
             best = held.tile([P, N // PASSAGE], F32, name="best%d" % b)
             nc.vector.tensor_reduce(
-                out=best[:], in_=turned[:].rearrange("p (j s) -> p j s", s=PASSAGE), axis=X, op=MAX
+                out=best[:], in_=turned[:].rearrange("p (x j y) -> p j x y", x=4, y=2 * QUAD), axis=XY, op=MAX
             )
             nc.sync.dma_start(out[b], best[:])

@@ -32,8 +32,13 @@ ZERO_PIECES = 4
 CHUNKS = (640, 640, 384, 256, 128)
 QUERIES_ON_GPSIMD = (128, 128, 128, 0)
 QUAD = 4
-SIDE_BY_SIDE = (("k", 0), ("q", 0), ("q", 1), ("k", 1), ("q", 2), ("k", 2), ("k", 3), ("q", 3))
-RUN = 512
+RUNS = (
+    (("q", 0), ("v", 0), ("v", 1), ("s", 0)),
+    (("s", 1), ("q", 1), ("v", 2), ("v", 3)),
+    (("q", 2), ("s", 2)),
+    (("s", 3),),
+    (("q", 3),),
+)
 
 
 def tile_attend_maxsim_tskb_kernel(tc, qT, kT, ts, kb, offs, out):
@@ -63,7 +68,7 @@ def tile_attend_maxsim_tskb_kernel(tc, qT, kT, ts, kb, offs, out):
             first = first + width
         q_raws = []
         for b in range(B):
-            q_raw = held.tile([P, PACK, NQ], F32, name="q_raw%d" % b, tag="q_raw%d" % b)
+            q_raw = held.tile([P, PACK, NQ], F32, name="q_raw%d" % b, tag="q_raw%d" % b, align_bytes=64)
             nc.sync.dma_start(q_raw[:], qT[b].rearrange("(p t) q -> p t q", t=PACK))
             q_raws.append(q_raw)
 
@@ -74,10 +79,11 @@ def tile_attend_maxsim_tskb_kernel(tc, qT, kT, ts, kb, offs, out):
         turned_rows = []
         for i, (name, win) in enumerate((("ts", ts_win), ("kb", kb_win))):
             values = held.tile([P, B * N], F32, name=name + "_picked")
-            nc.vector.tensor_copy(
-                values[:].bitcast(U32).rearrange("p (b x m i) -> p b m x i", b=B, x=4, i=QUAD),
-                win[:].bitcast(U32).indirect(offsets[:]),
-            )
+            for b in range(B):
+                nc.vector.tensor_copy(
+                    values[:, b * N : (b + 1) * N].bitcast(U32).rearrange("p (a h m i) -> p m h a i", a=2, h=2, i=QUAD),
+                    win[:].bitcast(U32).indirect(offsets[:, b * LIST_COLS : (b + 1) * LIST_COLS]),
+                )
             for part in range(2):
                 bank = psum.tile([P, PER_BANK, P], F32, name="bank", tag="bank%d" % (B + 2 * i + part))
                 for j in range(PER_BANK):
@@ -103,14 +109,16 @@ def tile_attend_maxsim_tskb_kernel(tc, qT, kT, ts, kb, offs, out):
         for i, turned_row in enumerate(turned_rows):
             nc.vector.tensor_copy(cols[:, i // 2, PER_BANK * (i % 2) : PER_BANK * (i % 2 + 1)], turned_row)
 
-        def gather_keys(b, woven):
-            listed = offsets[:, b * LIST_COLS : (b + 1) * LIST_COLS]
-            flat = woven.rearrange("p n t -> p (n t)")
-            dst = flat.bitcast(U32).rearrange("p (h a m w) -> p a m h w", h=2, a=2, w=2 * QUAD)
-            nc.vector.tensor_copy(dst[:, 0], words[:].rearrange("p n t -> p (n t)").bitcast(U32).indirect(listed))
+        def gather_keys(b, on_vector, on_scalar):
+            listed = offsets[:, b * LIST_COLS : (b + 2) * LIST_COLS]
+            dst = on_vector.rearrange("p n t -> p (n t)").bitcast(U32)
+            nc.vector.tensor_copy(
+                dst.rearrange("p (b h m w) -> p b m h w", b=2, h=2, w=2 * QUAD),
+                words[:].rearrange("p n t -> p (n t)").bitcast(U32).indirect(listed),
+            )
             for h in range(2):
                 nc.scalar.activation(
-                    flat[:, (2 * h + 1) * N : (2 * h + 2) * N],
+                    on_scalar.rearrange("p (b h n) t -> p h b (n t)", b=2, h=2)[:, h],
                     halves[h][:].rearrange("p n t -> p (n t)").indirect(listed),
                     COPY,
                 )
@@ -127,40 +135,37 @@ def tile_attend_maxsim_tskb_kernel(tc, qT, kT, ts, kb, offs, out):
                     COPY,
                 )
 
-        columns = B * (N + NQ)
-        woven = held.tile([P, columns, PACK], BF16, name="woven", tag="woven", align_bytes=64)
-        codes = held.tile([P, columns], U32, name="codes", align_bytes=64)
-        scales = held.tile([P, columns], U8, name="scales", align_bytes=64)
-        place = {}
-        first = 0
-        for kind, b in SIDE_BY_SIDE:
-            width = N if kind == "k" else NQ
-            place[(kind, b)] = slice(first, first + width)
-            first = first + width
+        woven = held.tile([P, B * (N + NQ), PACK], BF16, name="woven", tag="woven", align_bytes=64)
+        place = {member: i * P for i, member in enumerate(member for run in RUNS for member in run)}
+        for b in range(0, B, 2):
+            v, s = place[("v", b)], place[("s", b)]
+            gather_keys(b, woven[:, v : v + 2 * P, :], woven[:, s : s + 2 * P, :])
         for b in range(B):
-            gather_keys(b, woven[:, place[("k", b)], :])
-        for b in range(B):
-            weave_queries(b, woven[:, place[("q", b)], :])
-        for first in range(0, columns, RUN):
-            cut = slice(first, first + RUN)
+            weave_queries(b, woven[:, place[("q", b)] : place[("q", b)] + NQ, :])
+        operands = {}
+        for r, run in enumerate(RUNS):
+            tag = {3: "q_raw2"}.get(r, "codes%d" % r)
+            codes = held.tile([P, len(run) * P], U32, name="codes%d" % r, tag=tag, align_bytes=64)
+            scales = held.tile([P, len(run) * P], U8, name="scales%d" % r, align_bytes=64)
+            first = place[run[0]]
             nc.vector.quantize_mx(
-                out=codes[:, cut].bitcast(FP8X4),
-                scales=scales[:, cut],
-                in_=woven[:, cut, :].rearrange("p n t -> p (n t)"),
+                out=codes[:].bitcast(FP8X4),
+                scales=scales[:],
+                in_=woven[:, first : first + len(run) * P, :].rearrange("p n t -> p (n t)"),
             )
-        operands = {member: (codes[:, cut], scales[:, cut]) for member, cut in place.items()}
+            for i, member in enumerate(run):
+                operands[member] = (codes[:, i * P : (i + 1) * P], scales[:, i * P : (i + 1) * P])
 
         sums = []
         for b in range(B):
             q_codes, q_scales = operands[("q", b)]
-            k_codes, k_scales = operands[("k", b)]
             acc = psum.tile([P, HALVES, NQ], F32, name="acc%d" % b, tag="bank%d" % b)
             for half in range(HALVES):
-                slots = slice(half * P, (half + 1) * P)
+                k_codes, k_scales = operands[("vs"[half], b)]
                 nc.tensor.matmul_mx(
                     out=acc[:, half, :],
-                    lhsT=k_codes[:, slots].bitcast(FP8X4),
-                    lhsT_scale=k_scales[:, slots],
+                    lhsT=k_codes.bitcast(FP8X4),
+                    lhsT_scale=k_scales,
                     rhs=q_codes.bitcast(FP8X4),
                     rhs_scale=q_scales,
                     start=True,
@@ -168,7 +173,7 @@ def tile_attend_maxsim_tskb_kernel(tc, qT, kT, ts, kb, offs, out):
                 )
             sums.append(acc)
 
-        scored_all = held.tile([P, B * HALVES, NQ], F32, name="scored", tag="woven", align_bytes=64)
+        scored_all = held.tile([P, B * HALVES, NQ], F32, name="scored", tag="q_raw3", align_bytes=64)
         for b in range(B):
             turned = psum.tile([P, N], F32, name="turned%d" % b, tag="bank%d" % (B + b))
             for half in range(HALVES):

@@ -15,7 +15,7 @@ IDENT = mybir.ActivationFunctionType.Identity
 MAX = mybir.AluOpType.max
 MULT = mybir.AluOpType.mult
 ADD = mybir.AluOpType.add
-XY = mybir.AxisListType.XY
+X = mybir.AxisListType.X
 
 B, N, T, D, NQ = 4, 256, 2048, 512, 128
 PASSAGE = 32
@@ -30,7 +30,9 @@ ROW = P - 1
 ZERO_PIECES = 4
 
 CHUNKS = (640, 640, 384, 256, 128)
-QUERIES_ON_GPSIMD = (128, 128, 128, 0)
+QUERIES_ON_GPSIMD = (128, 128, 0, 0)
+QUERIES_ON_VECTOR = (0, 0, 128, 0)
+EARLY = 1280
 QUAD = 4
 RUNS = (
     (("q", 0), ("v", 0), ("v", 1), ("s", 0)),
@@ -78,17 +80,17 @@ def tile_attend_maxsim_tskb_kernel(tc, qT, kT, ts, kb, offs, out):
 
         turned_rows = []
         for i, (name, win) in enumerate((("ts", ts_win), ("kb", kb_win))):
-            values = held.tile([P, B * N], F32, name=name + "_picked")
-            for b in range(B):
-                nc.vector.tensor_copy(
-                    values[:, b * N : (b + 1) * N].bitcast(U32).rearrange("p (a h m i) -> p m h a i", a=2, h=2, i=QUAD),
-                    win[:].bitcast(U32).indirect(offsets[:, b * LIST_COLS : (b + 1) * LIST_COLS]),
-                )
+            listed = held.tile([P, B * N], F32, name=name + "_listed")
+            nc.vector.tensor_copy(listed[:], win[:].indirect(offsets[:]))
+            values = held.tile([P, B, HALVES, P], F32, name=name + "_by_slot")
+            tokens = listed[:].rearrange("p (b m h a i) -> p a b m h i", b=B, h=2, a=2, i=QUAD)
+            nc.vector.tensor_copy(values[:, :, 0, :].rearrange("p b (m h i) -> p b m h i", h=2, i=QUAD), tokens[:, 0])
+            nc.vector.tensor_copy(values[:, :, 1, :].rearrange("p b (h m i) -> p b m h i", h=2, i=QUAD), tokens[:, 1])
             for part in range(2):
                 bank = psum.tile([P, PER_BANK, P], F32, name="bank", tag="bank%d" % (B + 2 * i + part))
                 for j in range(PER_BANK):
                     block = PER_BANK * part + j
-                    nc.tensor.transpose(bank[:, j, :], values[:, block * P : (block + 1) * P], ident[:])
+                    nc.tensor.transpose(bank[:, j, :], values[:, block // HALVES, block % HALVES, :], ident[:])
                 turned_rows.append(bank[:, :, ROW])
 
         words = held.tile([P, T // 2, PACK], BF16, name="words")
@@ -100,26 +102,31 @@ def tile_attend_maxsim_tskb_kernel(tc, qT, kT, ts, kb, offs, out):
                 COPY,
             )
             for h in range(2):
-                nc.vector.tensor_copy(
-                    halves[h][:, first // 4 : (first + width) // 4, :].rearrange("p (m i) t -> p m t i", i=QUAD),
-                    raw[:].rearrange("p t (m h a i) -> p h a m t i", h=2, a=2, i=QUAD)[:, h, 1],
-                )
+                dst = halves[h][:, first // 4 : (first + width) // 4, :].rearrange("p (m i) t -> p m t i", i=QUAD)
+                src = raw[:].rearrange("p t (m h a i) -> p h a m t i", h=2, a=2, i=QUAD)[:, h, 1]
+                if h == 0 and first < EARLY:
+                    nc.scalar.activation(dst, src, COPY)
+                else:
+                    nc.vector.tensor_copy(dst, src)
 
         cols = held.tile([P, 2, B * HALVES], F32, name="cols", tag="raw%d" % (len(CHUNKS) - 3))
         for i, turned_row in enumerate(turned_rows):
             nc.vector.tensor_copy(cols[:, i // 2, PER_BANK * (i % 2) : PER_BANK * (i % 2 + 1)], turned_row)
 
         def gather_keys(b, on_vector, on_scalar):
-            listed = offsets[:, b * LIST_COLS : (b + 2) * LIST_COLS]
-            dst = on_vector.rearrange("p n t -> p (n t)").bitcast(U32)
             nc.vector.tensor_copy(
-                dst.rearrange("p (b h m w) -> p b m h w", b=2, h=2, w=2 * QUAD),
-                words[:].rearrange("p n t -> p (n t)").bitcast(U32).indirect(listed),
+                on_vector.rearrange("p n t -> p (n t)").bitcast(U32),
+                words[:].rearrange("p n t -> p (n t)").bitcast(U32).indirect(
+                    offsets[:, b * LIST_COLS : (b + 2) * LIST_COLS]
+                ),
             )
-            for h in range(2):
+            for i in range(4):
+                search = b + i // 2
                 nc.scalar.activation(
-                    on_scalar.rearrange("p (b h n) t -> p h b (n t)", b=2, h=2)[:, h],
-                    halves[h][:].rearrange("p n t -> p (n t)").indirect(listed),
+                    on_scalar.rearrange("p n t -> p (n t)")[:, i * N : (i + 1) * N],
+                    halves[i % 2][:].rearrange("p n t -> p (n t)").indirect(
+                        offsets[:, search * LIST_COLS : (search + 1) * LIST_COLS]
+                    ),
                     COPY,
                 )
 
@@ -128,6 +135,13 @@ def tile_attend_maxsim_tskb_kernel(tc, qT, kT, ts, kb, offs, out):
             if split > 0:
                 src = q_raws[b][:, :, 0:split].rearrange("p t q -> p q t")
                 nc.gpsimd.tensor_scalar(woven[:, 0:split, :], src, 1.0, 0.0, MULT, ADD)
+            if QUERIES_ON_VECTOR[b] > 0:
+                cut = slice(split, split + QUERIES_ON_VECTOR[b])
+                nc.vector.tensor_copy(
+                    woven[:, cut, :].rearrange("p (c i) t -> p c t i", i=4),
+                    q_raws[b][:, :, cut].rearrange("p t (c i) -> p c t i", i=4),
+                )
+                split = cut.stop
             if split < NQ:
                 nc.scalar.activation(
                     woven[:, split:NQ, :].rearrange("p (c i) t -> p c t i", i=4),
@@ -184,9 +198,17 @@ def tile_attend_maxsim_tskb_kernel(tc, qT, kT, ts, kb, offs, out):
                     nc.vector.tensor_scalar(scored, sums[b][:, half, :], scale, bias, MULT, ADD)
                 else:
                     nc.scalar.activation(scored, sums[b][:, half, :], IDENT, bias=bias, scale=scale)
-                nc.tensor.transpose(turned[:, half * P : (half + 1) * P], scored, ident[:])
+                places = turned[:].rearrange("p (j a h y) -> p a j h y", a=2, h=2, y=2 * QUAD)[:, half]
+                if half == 0:
+                    nc.tensor.transpose(places, scored, ident[:].rearrange("p (j h y) -> p j h y", h=2, y=2 * QUAD))
+                else:
+                    nc.tensor.transpose(
+                        places.rearrange("p j h y -> p h j y"),
+                        scored,
+                        ident[:].rearrange("p (h j y) -> p h j y", h=2, y=2 * QUAD),
+                    )
             best = held.tile([P, N // PASSAGE], F32, name="best%d" % b)
             nc.vector.tensor_reduce(
-                out=best[:], in_=turned[:].rearrange("p (x j y) -> p j x y", x=4, y=2 * QUAD), axis=XY, op=MAX
+                out=best[:], in_=turned[:].rearrange("p (j y) -> p j y", y=PASSAGE), axis=X, op=MAX
             )
             nc.sync.dma_start(out[b], best[:])

@@ -31,15 +31,14 @@ ZERO_PIECES = 4
 
 CHUNKS = (640, 640, 384, 256, 128)
 QUERIES_ON_GPSIMD = (128, 128, 0, 0)
-QUERIES_ON_VECTOR = (0, 0, 128, 0)
 EARLY = 1280
 QUAD = 4
 RUNS = (
     (("q", 0), ("v", 0), ("v", 1), ("s", 0)),
     (("s", 1), ("q", 1), ("v", 2), ("v", 3)),
     (("q", 2), ("s", 2)),
-    (("s", 3),),
     (("q", 3),),
+    (("s", 3),),
 )
 
 
@@ -47,6 +46,7 @@ def tile_attend_maxsim_tskb_kernel(tc, qT, kT, ts, kb, offs, out):
     nc = tc.nc
     with ExitStack() as ctx:
         held = ctx.enter_context(tc.tile_pool(name="held", bufs=1))
+        reused = ctx.enter_context(tc.tile_pool(name="reused", bufs=1))
         psum = ctx.enter_context(tc.psum_pool(name="psum", bufs=1))
 
         offsets = held.tile([P, B * LIST_COLS], U16, name="offsets")
@@ -70,7 +70,10 @@ def tile_attend_maxsim_tskb_kernel(tc, qT, kT, ts, kb, offs, out):
             first = first + width
         q_raws = []
         for b in range(B):
-            q_raw = held.tile([P, PACK, NQ], F32, name="q_raw%d" % b, tag="q_raw%d" % b, align_bytes=64)
+            if b < B - 1:
+                q_raw = held.tile([P, PACK, NQ], F32, name="q_raw%d" % b)
+            else:
+                q_raw = reused.tile([P, PACK, NQ], F32, name="q_last", offset=0, align_bytes=64)
             nc.sync.dma_start(q_raw[:], qT[b].rearrange("(p t) q -> p t q", t=PACK))
             q_raws.append(q_raw)
 
@@ -122,26 +125,19 @@ def tile_attend_maxsim_tskb_kernel(tc, qT, kT, ts, kb, offs, out):
             )
             for i in range(4):
                 search = b + i // 2
-                nc.scalar.activation(
-                    on_scalar.rearrange("p n t -> p (n t)")[:, i * N : (i + 1) * N],
-                    halves[i % 2][:].rearrange("p n t -> p (n t)").indirect(
-                        offsets[:, search * LIST_COLS : (search + 1) * LIST_COLS]
-                    ),
-                    COPY,
-                )
+                dst = on_scalar[i // 2].rearrange("p n t -> p (n t)")[:, (i % 2) * N : (i % 2 + 1) * N]
+                src = halves[i % 2][:].rearrange("p n t -> p (n t)")
+                listed = offsets[:, search * LIST_COLS : (search + 1) * LIST_COLS]
+                if i % 2 == 1 and search >= 2:
+                    nc.vector.tensor_copy(dst, src.indirect(listed))
+                else:
+                    nc.scalar.activation(dst, src.indirect(listed), COPY)
 
         def weave_queries(b, woven):
             split = QUERIES_ON_GPSIMD[b]
             if split > 0:
                 src = q_raws[b][:, :, 0:split].rearrange("p t q -> p q t")
                 nc.gpsimd.tensor_scalar(woven[:, 0:split, :], src, 1.0, 0.0, MULT, ADD)
-            if QUERIES_ON_VECTOR[b] > 0:
-                cut = slice(split, split + QUERIES_ON_VECTOR[b])
-                nc.vector.tensor_copy(
-                    woven[:, cut, :].rearrange("p (c i) t -> p c t i", i=4),
-                    q_raws[b][:, :, cut].rearrange("p t (c i) -> p c t i", i=4),
-                )
-                split = cut.stop
             if split < NQ:
                 nc.scalar.activation(
                     woven[:, split:NQ, :].rearrange("p (c i) t -> p c t i", i=4),
@@ -152,14 +148,17 @@ def tile_attend_maxsim_tskb_kernel(tc, qT, kT, ts, kb, offs, out):
         woven = held.tile([P, B * (N + NQ), PACK], BF16, name="woven", tag="woven", align_bytes=64)
         place = {member: i * P for i, member in enumerate(member for run in RUNS for member in run)}
         for b in range(0, B, 2):
-            v, s = place[("v", b)], place[("s", b)]
-            gather_keys(b, woven[:, v : v + 2 * P, :], woven[:, s : s + 2 * P, :])
+            v = place[("v", b)]
+            blocks = [woven[:, place[("s", b + i)] : place[("s", b + i)] + P, :] for i in range(2)]
+            gather_keys(b, woven[:, v : v + 2 * P, :], blocks)
         for b in range(B):
             weave_queries(b, woven[:, place[("q", b)] : place[("q", b)] + NQ, :])
         operands = {}
         for r, run in enumerate(RUNS):
-            tag = {3: "q_raw2"}.get(r, "codes%d" % r)
-            codes = held.tile([P, len(run) * P], U32, name="codes%d" % r, tag=tag, align_bytes=64)
+            if r < len(RUNS) - 1:
+                codes = held.tile([P, len(run) * P], U32, name="codes%d" % r, align_bytes=64)
+            else:
+                codes = reused.tile([P, P], U32, name="codes_last", offset=0, align_bytes=64)
             scales = held.tile([P, len(run) * P], U8, name="scales%d" % r, align_bytes=64)
             first = place[run[0]]
             nc.vector.quantize_mx(
@@ -187,7 +186,7 @@ def tile_attend_maxsim_tskb_kernel(tc, qT, kT, ts, kb, offs, out):
                 )
             sums.append(acc)
 
-        scored_all = held.tile([P, B * HALVES, NQ], F32, name="scored", tag="q_raw3", align_bytes=64)
+        scored_all = reused.tile([P, B * HALVES, NQ], F32, name="scored", offset=4 * P, align_bytes=64)
         for b in range(B):
             turned = psum.tile([P, N], F32, name="turned%d" % b, tag="bank%d" % (B + b))
             for half in range(HALVES):

from contextlib import ExitStack

import concourse.mybir as mybir
from concourse.masks import make_identity

F32 = mybir.dt.float32
BF16 = mybir.dt.bfloat16
U32 = mybir.dt.uint32
I32 = mybir.dt.int32
U16 = mybir.dt.uint16
U8 = mybir.dt.uint8
FP8X4 = mybir.dt.float8_e4m3fn_x4
COPY = mybir.ActivationFunctionType.Copy
IDENT = mybir.ActivationFunctionType.Identity
MAX = mybir.AluOpType.max
MULT = mybir.AluOpType.mult
ADD = mybir.AluOpType.add
X = mybir.AxisListType.X

B, N, T, D, NQ = 4, 256, 2048, 512, 128
PASSAGE = 32
P = 128
PACK = 4
FLOPS = 2 * B * NQ * N * D
HALVES = N // P
LIST_COLS = N // 16
PER_BANK = 4

ROW = P - 1
ZERO_PIECES = 4

CHUNKS = (640, 640, 384, 256, 128)
QUERIES_ON_GPSIMD = (128, 128, 0, 0)
EARLY = 1280
QUAD = 4
RUNS = (
    (("q", 0), ("v", 0), ("v", 1), ("s", 0)),
    (("s", 1), ("q", 1), ("v", 2), ("v", 3)),
    (("q", 2), ("s", 2)),
    (("q", 3),),
    (("s", 3),),
)


def tile_attend_maxsim_tskb_kernel(tc, qT, kT, ts, kb, offs, out):
    nc = tc.nc
    with ExitStack() as ctx:
        held = ctx.enter_context(tc.tile_pool(name="held", bufs=1))
        reused = ctx.enter_context(tc.tile_pool(name="reused", bufs=1))
        psum = ctx.enter_context(tc.psum_pool(name="psum", bufs=1))

        offsets = held.tile([P, B * LIST_COLS], U16, name="offsets")
        nc.sync.dma_start(offsets[:], offs)

        ts_win = held.tile([P, T], F32, name="ts_win")
        kb_win = held.tile([P, T], F32, name="kb_win")
        nc.scalar.dma_start(ts_win[ROW:P, :], ts[0:1, :])
        nc.scalar.dma_start(kb_win[ROW:P, :], kb[0:1, :])
        nc.vector.memset(ts_win[0:ROW, :], 0.0)
        for piece in range(ZERO_PIECES):
            nc.gpsimd.memset(kb_win[0:ROW, piece * T // ZERO_PIECES : (piece + 1) * T // ZERO_PIECES], 0.0)

        k_rows = kT.rearrange("(p t) w -> p t w", t=PACK)
        loaded = []
        first = 0
        for c, width in enumerate(CHUNKS):
            raw = held.tile([P, PACK, width], F32, name="raw%d" % c, tag="raw%d" % c)
            nc.sync.dma_start(raw[:], k_rows[:, :, first : first + width])
            loaded.append((raw, first, width))
            first = first + width
        q_raws = []
        for b in range(B):
            if b < B - 1:
                q_raw = held.tile([P, PACK, NQ], F32, name="q_raw%d" % b)
            else:
                q_raw = reused.tile([P, PACK, NQ], F32, name="q_last", offset=0, align_bytes=64)
            nc.sync.dma_start(q_raw[:], qT[b].rearrange("(p t) q -> p t q", t=PACK))
            q_raws.append(q_raw)

        ident = held.tile([P, P], F32, name="ident")
        nc.vector.memset(ident[:], 0.0)
        make_identity(nc, ident[:], nomemset=True)

        turned_rows = []
        for i, (name, win) in enumerate((("ts", ts_win), ("kb", kb_win))):
            listed = held.tile([P, B * N], F32, name=name + "_listed")
            nc.vector.tensor_copy(listed[:], win[:].indirect(offsets[:]))
            values = held.tile([P, B, HALVES, P], F32, name=name + "_by_slot")
            tokens = listed[:].rearrange("p (b m h a i) -> p a b m h i", b=B, h=2, a=2, i=QUAD)
            nc.vector.tensor_copy(values[:, :, 0, :].rearrange("p b (m h i) -> p b m h i", h=2, i=QUAD), tokens[:, 0])
            nc.vector.tensor_copy(values[:, :, 1, :].rearrange("p b (h m i) -> p b m h i", h=2, i=QUAD), tokens[:, 1])
            for part in range(2):
                bank = psum.tile([P, PER_BANK, P], F32, name="bank", tag="bank%d" % (B + 2 * i + part))
                for j in range(PER_BANK):
                    block = PER_BANK * part + j
                    nc.tensor.transpose(bank[:, j, :], values[:, block // HALVES, block % HALVES, :], ident[:])
                turned_rows.append(bank[:, :, ROW])

        words = held.tile([P, T // 2, PACK], BF16, name="words")
        halves = [held.tile([P, T // 4, PACK], BF16, name="halves%d" % h) for h in range(2)]
        for raw, first, width in loaded:
            nc.scalar.activation(
                words[:, first // 2 : (first + width) // 2, :].rearrange("p (m i) t -> p m t i", i=QUAD),
                raw[:].rearrange("p t (m a i) -> p a m t i", a=2, i=QUAD)[:, 0],
                COPY,
            )
            for h in range(2):
                dst = halves[h][:, first // 4 : (first + width) // 4, :].rearrange("p (m i) t -> p m t i", i=QUAD)
                src = raw[:].rearrange("p t (m h a i) -> p h a m t i", h=2, a=2, i=QUAD)[:, h, 1]
                if h == 0 and first < EARLY:
                    nc.scalar.activation(dst, src, COPY)
                else:
                    nc.vector.tensor_copy(dst, src)

        cols = held.tile([P, 2, B * HALVES], F32, name="cols", tag="raw%d" % (len(CHUNKS) - 3))
        for i, turned_row in enumerate(turned_rows):
            nc.vector.tensor_copy(cols[:, i // 2, PER_BANK * (i % 2) : PER_BANK * (i % 2 + 1)], turned_row)

        def gather_keys(b, on_vector, on_scalar):
            nc.vector.tensor_copy(
                on_vector.rearrange("p n t -> p (n t)").bitcast(U32),
                words[:].rearrange("p n t -> p (n t)").bitcast(U32).indirect(
                    offsets[:, b * LIST_COLS : (b + 2) * LIST_COLS]
                ),
            )
            for i in range(4):
                search = b + i // 2
                dst = on_scalar[i // 2].rearrange("p n t -> p (n t)")[:, (i % 2) * N : (i % 2 + 1) * N]
                src = halves[i % 2][:].rearrange("p n t -> p (n t)")
                listed = offsets[:, search * LIST_COLS : (search + 1) * LIST_COLS]
                if i % 2 == 1 and search >= 2:
                    nc.vector.tensor_copy(dst, src.indirect(listed))
                else:
                    nc.scalar.activation(dst, src.indirect(listed), COPY)

        def weave_queries(b, woven):
            split = QUERIES_ON_GPSIMD[b]
            if split > 0:
                src = q_raws[b][:, :, 0:split].rearrange("p t q -> p q t")
                nc.gpsimd.tensor_scalar(woven[:, 0:split, :], src, 1.0, 0.0, MULT, ADD)
            if split < NQ:
                nc.scalar.activation(
                    woven[:, split:NQ, :].rearrange("p (c i) t -> p c t i", i=4),
                    q_raws[b][:, :, split:NQ].rearrange("p t (c i) -> p c t i", i=4),
                    COPY,
                )

        woven = held.tile([P, B * (N + NQ), PACK], BF16, name="woven", tag="woven", align_bytes=64)
        place = {member: i * P for i, member in enumerate(member for run in RUNS for member in run)}
        for b in range(0, B, 2):
            v = place[("v", b)]
            blocks = [woven[:, place[("s", b + i)] : place[("s", b + i)] + P, :] for i in range(2)]
            gather_keys(b, woven[:, v : v + 2 * P, :], blocks)
        for b in range(B):
            weave_queries(b, woven[:, place[("q", b)] : place[("q", b)] + NQ, :])
        operands = {}
        for r, run in enumerate(RUNS):
            if r < len(RUNS) - 1:
                codes = held.tile([P, len(run) * P], U32, name="codes%d" % r, align_bytes=64)
            else:
                codes = reused.tile([P, P], U32, name="codes_last", offset=0, align_bytes=64)
            scales = held.tile([P, len(run) * P], U8, name="scales%d" % r, align_bytes=64)
            first = place[run[0]]
            nc.vector.quantize_mx(
                out=codes[:].bitcast(FP8X4),
                scales=scales[:],
                in_=woven[:, first : first + len(run) * P, :].rearrange("p n t -> p (n t)"),
            )
            for i, member in enumerate(run):
                operands[member] = (codes[:, i * P : (i + 1) * P], scales[:, i * P : (i + 1) * P])

        sums = []
        for b in range(B):
            q_codes, q_scales = operands[("q", b)]
            acc = psum.tile([P, HALVES, NQ], F32, name="acc%d" % b, tag="bank%d" % b)
            for half in range(HALVES):
                k_codes, k_scales = operands[("vs"[half], b)]
                nc.tensor.matmul_mx(
                    out=acc[:, half, :],
                    lhsT=k_codes.bitcast(FP8X4),
                    lhsT_scale=k_scales,
                    rhs=q_codes.bitcast(FP8X4),
                    rhs_scale=q_scales,
                    start=True,
                    stop=True,
                )
            sums.append(acc)

        scored_all = reused.tile([P, B * HALVES, NQ], F32, name="scored", offset=4 * P, align_bytes=64)
        for b in range(B):
            turned = psum.tile([P, N], F32, name="turned%d" % b, tag="bank%d" % (B + b))
            for half in range(HALVES):
                block = HALVES * b + half
                scored = scored_all[:, block, :]
                scale, bias = cols[:, 0, block : block + 1], cols[:, 1, block : block + 1]
                if b == B - 1:
                    nc.vector.tensor_scalar(scored, sums[b][:, half, :], scale, bias, MULT, ADD)
                else:
                    nc.scalar.activation(scored, sums[b][:, half, :], IDENT, bias=bias, scale=scale)
                places = turned[:].rearrange("p (j a h y) -> p a j h y", a=2, h=2, y=2 * QUAD)[:, half]
                if half == 0:
                    nc.tensor.transpose(places, scored, ident[:].rearrange("p (j h y) -> p j h y", h=2, y=2 * QUAD))
                else:
                    nc.tensor.transpose(
                        places.rearrange("p j h y -> p h j y"),
                        scored,
                        ident[:].rearrange("p (h j y) -> p h j y", h=2, y=2 * QUAD),
                    )
            best = held.tile([P, N // PASSAGE], F32, name="best%d" % b)
            nc.vector.tensor_reduce(
                out=best[:], in_=turned[:].rearrange("p (j y) -> p j y", y=PASSAGE), axis=X, op=MAX
            )
            nc.sync.dma_start(out[b], best[:])
